import numpy as np
import ml_dtypes


def mxq(x, axis, fmt="e4m3"):
    dtype, down = {"e4m3": (ml_dtypes.float8_e4m3fn, 7), "e5m2": (ml_dtypes.float8_e5m2, 14)}[fmt]
    v = np.moveaxis(np.asarray(x, np.float32).astype(ml_dtypes.bfloat16).astype(np.float64), axis, -1)
    blocks = v.reshape(v.shape[:-1] + (-1, 32))
    amax = np.abs(blocks).max(-1, keepdims=True)
    byte = np.maximum(np.where(amax > 0, np.frexp(amax)[1] - 1 + 127, 0) - down, 1)
    scale = np.exp2(byte - 127.0)
    codes = (blocks / scale).astype(np.float32).astype(dtype).astype(np.float64)
    return np.moveaxis((codes * scale).reshape(v.shape), -1, axis)


WIDE = False


def mx_kscale(k):
    if not WIDE:
        return np.ones(k)
    levels = np.array([10, -10, 5, -5, 0])
    if k % 512:
        return np.exp2(np.random.permutation(np.resize(levels, k // 32))).repeat(32)
    a = np.empty((k // 512, 16))
    for p in range(k // 512):
        a[p, :8] = np.random.permutation(np.resize(levels, 8))
        for g in range(8):
            far = levels[np.abs(levels - a[p, g]) >= 10]
            a[p, g + 8] = far[np.random.randint(len(far))]
    return np.exp2(a.ravel()).repeat(32)


def f64(x):
    return np.asarray(x).astype(np.float64)


def striped(idx):
    return np.tile(idx.reshape(-1, 16).T, (8, 1)).astype(np.uint16)


def unstriped(offs):
    return offs[:16].T.reshape(-1).astype(np.int64)


E2M1 = np.array([0.0, 0.5, 1.0, 1.5, 2.0, 3.0, 4.0, 6.0, -0.0, -0.5, -1.0, -1.5, -2.0, -3.0, -4.0, -6.0])


def pack_weight(w, fmt):
    k, n = w.shape
    w = f64(np.asarray(w, np.float32).astype(ml_dtypes.bfloat16)).reshape(k // 32, 32, n)
    amax = np.abs(w).max(1)
    if fmt == "e4m3":
        byte = np.frexp(amax)[1] - 1 + 127 - 7
    else:
        mant, ex = np.frexp(amax / 6.0)
        byte = np.where(mant > 0.5, ex, ex - 1) + 127
    byte = np.clip(np.where(amax > 0, byte, 1), 1, 254)
    scaled = (w * np.exp2(127.0 - byte)[:, None, :]).reshape(k, n).astype(np.float32)
    by_word = np.ascontiguousarray(scaled.reshape(k // 512, 128, 4, n).transpose(0, 1, 3, 2))
    if fmt == "e4m3":
        words = by_word.astype(ml_dtypes.float8_e4m3fn).view(np.uint8)
    else:
        c = by_word.astype(ml_dtypes.float4_e2m1fn).view(np.uint8) & 0xF
        words = (c[..., 0::2] | (c[..., 1::2] << 4)).reshape(k // 512, 128, 2 * n)
    return np.ascontiguousarray(words), np.ascontiguousarray(byte.astype(np.uint8).reshape(k // 512, 16, n))


def unpack_weight(words, scales, fmt):
    g, _, n = scales.shape
    words = np.ascontiguousarray(words).reshape(g, 128, n, -1)
    if fmt == "e4m3":
        vals = words.view(ml_dtypes.float8_e4m3fn).astype(np.float64)
    else:
        nib = np.empty((g, 128, n, 4), np.uint8)
        nib[..., 0::2] = words & 0xF
        nib[..., 1::2] = words >> 4
        vals = E2M1[nib]
    vals = vals * np.repeat(np.exp2(scales.astype(np.float64) - 127.0), 8, axis=1)[..., None]
    return vals.transpose(0, 1, 3, 2).reshape(g * 512, n)


def gelu(v):
    return 0.5 * v * (1.0 + np.tanh(np.sqrt(2.0 / np.pi) * (v + 0.044715 * v**3)))


def bf(x):
    return np.asarray(x, np.float32).astype(ml_dtypes.bfloat16)


def planes(Y):
    n, m = Y.shape
    b = f64(bf(Y)).reshape(n // 32, 32, m)
    amax = np.abs(b).max(1)
    byte = np.clip(np.where(amax > 0, np.frexp(amax)[1] - 1 + 127 - 7, 1), 1, 254)
    codes = (b * np.exp2(127.0 - byte)[:, None, :]).reshape(n, m).astype(np.float32).astype(ml_dtypes.float8_e4m3fn).view(np.uint8)
    words = codes.reshape(n // 512, 128, 4, m).transpose(0, 1, 3, 2)
    return np.ascontiguousarray(words), np.ascontiguousarray(byte.astype(np.uint8).reshape(n // 512, 16, m))


K, H, N, T, S = 1024, 512, 1024, 4096, 1024

def setup_inputs():
    n = np.random.standard_normal
    s = mx_kscale(K)[:, None]
    u = mx_kscale(H)[:, None]
    tab_words, tab_scales = pack_weight(n((K, T)) * s, "e2m1")
    wb_words, wb_scales = pack_weight(n((K, H)) / np.sqrt(K) / s * u.T, "e4m3")
    wd_words, wd_scales = pack_weight(n((H, N)) / np.sqrt(H) / u, "e2m1")
    return {
        "tab_words": tab_words, "tab_scales": tab_scales,
        "offs": striped(np.random.permutation(T)[:S]),
        "offs2": striped(np.random.permutation(T)[:S]),
        "w1": (0.8 * n((K, H)) / np.sqrt(K) / s).astype(np.float32),
        "b1": (0.3 * n(H)).astype(np.float32),
        "wb_words": wb_words, "wb_scales": wb_scales,
        "wd_words": wd_words, "wd_scales": wd_scales,
        "gain": np.exp(0.8 * n(N)).astype(np.float32),
    }

def reference(tab_words, tab_scales, offs, offs2, w1, b1, wb_words, wb_scales, wd_words, wd_scales, gain):
    TW = unpack_weight(tab_words, tab_scales, "e2m1")
    v = TW[:, unstriped(offs)]
    v2 = TW[:, unstriped(offs2)]
    WB = unpack_weight(wb_words, wb_scales, "e4m3")
    WD = unpack_weight(wd_words, wd_scales, "e2m1")
    a = mxq(f64(w1), 0, "e4m3").T @ v
    t = np.tanh(a + f64(b1)[:, None])
    e = WB.T @ v2
    h = (1.0 - np.square(t)) * e
    y = f64(gain)[:, None] * (WD.T @ mxq(h, 0, "e4m3"))
    words, scales = planes(y)
    return y, words, scales

@@ -1,0 +1,314 @@
+from contextlib import ExitStack
+
+import concourse.mybir as mybir
+
+K, H, N, T, S = 1024, 512, 1024, 4096, 1024
+FLOPS = 2 * K * H * S * 2 + 2 * H * N * S
+
+F32 = mybir.dt.float32
+BF16 = mybir.dt.bfloat16
+I32 = mybir.dt.int32
+U32 = mybir.dt.uint32
+U16 = mybir.dt.uint16
+U8 = mybir.dt.uint8
+FP8X4 = mybir.dt.float8_e4m3fn_x4
+FP4X4 = mybir.dt.float4_e2m1fn_x4
+ACT = mybir.ActivationFunctionType
+ALU = mybir.AluOpType
+
+P = 128
+PACK = 4
+GROUP = P * PACK
+PASSES = K // GROUP
+GROUPS = N // GROUP
+HALF = S // 2
+QUARTER = S // 4
+BLOCK = 128
+SHIFT = 16
+
+
+def tile_list_cocitation_drift_backward_kernel(
+    tc, tab_words, tab_scales, offs, offs2, w1, b1, wb_words, wb_scales, wd_words, wd_scales, gain,
+    out_0, out_1, out_2,
+):
+    nc = tc.nc
+    with ExitStack() as ctx:
+        lists = ctx.enter_context(tc.tile_pool(name="lists", bufs=1))
+        pool = ctx.enter_context(tc.tile_pool(name="pool", bufs=1))
+        reuse = ctx.enter_context(tc.tile_pool(name="reuse", bufs=1))
+        psum = ctx.enter_context(tc.psum_pool(name="psum", bufs=1))
+
+        def sb(shape, dtype, name, tag=None):
+            return pool.tile(shape, dtype, name=name, tag=tag or name, align_bytes=64)
+
+        def placed(shape, dtype, name, offset):
+            return reuse.tile(shape, dtype, name=name, offset=offset, align_bytes=64)
+
+        idx = [lists.tile([P, S // 16], U16, name="idx%d" % n) for n in range(2)]
+
+        tab_sc = sb([P, T], U8, "tab_sc")
+        nc.vector.memset(tab_sc[:].bitcast(I32), 0)
+        wb_sc_raw = sb([P, PASSES * H], U8, "wb_sc_raw")
+        nc.vector.memset(wb_sc_raw[:].bitcast(I32), 0)
+
+        gain_raw = reuse.tile([P, GROUPS, 2 * PACK], F32, name="gain_raw", offset=8160, align_bytes=32)
+        nc.sync.dma_start(gain_raw[:, :, :PACK], gain.rearrange("(g p t) -> p g t", p=P, t=PACK))
+        nc.sync.dma_start(idx[0][:], offs)
+        nc.sync.dma_start(idx[1][:], offs2)
+        tab_rows = tab_scales.bitcast(I32).rearrange("a (q r) c -> r q a c", r=4)
+        for r in range(4):
+            nc.sync.dma_start(tab_sc[:].bitcast(I32)[r:P:SHIFT, :], tab_rows[r])
+
+        bias = sb([P, PACK], F32, "bias")
+        nc.gpsimd.dma_start(bias[:], b1.rearrange("(p t) -> p t", t=PACK))
+        wb_rows = wb_scales.bitcast(I32).rearrange("a (q r) c -> r q a c", r=4)
+        wd_rows = wd_scales[0].bitcast(I32).rearrange("(q r) c -> r q c", r=4)
+        for r in range(4):
+            nc.gpsimd.dma_start(
+                wb_sc_raw[:].bitcast(I32)[r:P:32, :].rearrange("q (a c) -> q a c", a=PASSES), wb_rows[r]
+            )
+
+        neg_gain = sb([P, GROUPS * PACK], F32, "neg_gain")
+        nc.scalar.activation(
+            neg_gain[:].rearrange("p (g t) -> p g t", t=PACK), gain_raw[:, :, :PACK], ACT.Copy, scale=-1.0
+        )
+
+        w1_rows = w1.rearrange("(a p j) c -> a p j c", p=P, j=PACK)
+        w1_codes, w1_sc = [], []
+        w1_bf = [sb([P, PACK, P, PACK], BF16, "w1_bf0"), sb([P, PACK, P, PACK], BF16, "w1_bf1")]
+
+        def load_w1(a, c, raw):
+            piece = raw.rearrange("p (j c) -> p j c", j=PACK)
+            nc.sync.dma_start(piece, w1_rows[a][:, :, c * H // 2 : (c + 1) * H // 2])
+            nc.scalar.activation(
+                w1_bf[a][:, :, c * P // 2 : (c + 1) * P // 2, :].rearrange("p t m j -> p m j t"),
+                piece.rearrange("p j (m t) -> p m j t", t=PACK),
+                ACT.Copy,
+            )
+
+        def quantise_w1(a):
+            w1_codes.append(sb([P, H], U32, "w1_codes%d" % a))
+            w1_sc.append(sb([P, H], U8, "w1_sc%d" % a))
+            nc.vector.quantize_mx(
+                out=w1_codes[a][:].bitcast(FP8X4),
+                scales=w1_sc[a][:],
+                in_=w1_bf[a][:].rearrange("p t m j -> p (t m j)"),
+            )
+
+        tab = []
+
+        def load_table(a, tile):
+            tab.append(tile)
+            nc.sync.dma_start(tab[a][:].bitcast(I32), tab_words[a].bitcast(I32))
+
+        piece_len = PACK * H // 2
+        w1_first = placed([P, piece_len], F32, "w1_first", 23552)
+        load_w1(0, 0, w1_first[:])
+        load_table(0, placed([P, T], U16, "tab0", 0))
+        w1_second = placed([P, piece_len], F32, "w1_second", 8192)
+        load_w1(0, 1, w1_second[:])
+        w1_rest = placed([P, 2 * piece_len], F32, "w1_rest", 16384)
+        for c in range(2):
+            load_w1(1, c, w1_rest[:, c * piece_len : (c + 1) * piece_len])
+        load_table(1, placed([P, T], U16, "tab1", 26624))
+        v_sc_hi = placed([P, 2 * S], U8, "v_sc_hi", 24576)
+        nc.vector.memset(v_sc_hi[:].bitcast(I32), 0)
+
+        v_sc = []
+        for n in range(2):
+            v_sc_lo = sb([P, S], U8, "v_sc_lo%d" % n)
+            nc.vector.tensor_copy(v_sc_lo[:], tab_sc[:].indirect(idx[n][:]))
+            moved = v_sc_hi[:, n * S : (n + 1) * S]
+            nc.sync.dma_start(moved.bitcast(I32)[0 : P - SHIFT, :], v_sc_lo[:].bitcast(I32)[SHIFT:P, :])
+            v_sc.append((v_sc_lo[:], moved))
+
+        def deal(out, in_):
+            nc.vector.tensor_copy(
+                out.rearrange("p (u t m) -> p u m t", t=PACK, m=P),
+                in_.rearrange("p (u m t) -> p u m t", t=PACK, m=P),
+            )
+
+        v = {}
+
+        def gather(n, a, half, tag=None, offset=None):
+            name = "v%d%d%d" % (n, a, half)
+            v[n, a, half] = sb([P, HALF], U16, name, tag) if offset is None else placed([P, HALF], U16, name, offset)
+            columns = slice(half * HALF // 16, (half + 1) * HALF // 16)
+            nc.vector.tensor_copy(v[n, a, half][:], tab[a][:].indirect(idx[n][:, columns]))
+
+        pre = {}
+
+        def hidden_matmuls(half):
+            entries = slice(half * HALF, (half + 1) * HALF)
+            for t in range(PACK):
+                pre[half, t] = psum.tile([P, HALF], F32, name="pre%d%d" % (half, t), tag="bank%d" % (half * PACK + t))
+            for a in range(PASSES):
+                for t in range(PACK):
+                    units = slice(t * P, (t + 1) * P)
+                    nc.tensor.matmul_mx(
+                        out=pre[half, t][:],
+                        lhsT=w1_codes[a][:, units].bitcast(FP8X4),
+                        lhsT_scale=w1_sc[a][:, units],
+                        rhs=v[0, a, half][:].bitcast(FP4X4),
+                        rhs_scale=v_sc[0][a][:, entries],
+                        start=(a == 0),
+                        stop=(a == PASSES - 1),
+                    )
+
+        for a in range(PASSES):
+            quantise_w1(a)
+            gather(0, a, 0)
+            gather(0, a, 1)
+        gather(1, 1, 0)
+
+        w_raw = placed([P, PASSES * H + N // 2], I32, "w_raw", 9216)
+        wb_raw = w_raw[:, : PASSES * H]
+        wd_raw = w_raw[:, PASSES * H :]
+        nc.sync.dma_start(
+            wb_raw.rearrange("p (a c) -> p a c", a=PASSES), wb_words.rearrange("a p c i -> p a (c i)").bitcast(I32)
+        )
+        nc.sync.dma_start(wd_raw, wd_words[0].bitcast(I32))
+        wd_sc_raw = placed([P, N], U8, "wd_sc_raw", 8192)
+        nc.vector.memset(wd_sc_raw[:].bitcast(I32), 0)
+        for r in range(4):
+            nc.sync.dma_start(wd_sc_raw[:].bitcast(I32)[r:P:32, :], wd_rows[r])
+
+        wb_sc = sb([P, PASSES * H], U8, "wb_sc", "w1_bf1")
+        deal(wb_sc[:], wb_sc_raw[:])
+        wb = sb([P, PASSES * H], I32, "wb")
+        deal(wb[:], wb_raw)
+        hidden_matmuls(0)
+        hidden_matmuls(1)
+        gather(1, 0, 0, "v010")
+        wd = sb([P, N], U16, "wd")
+        deal(wd[:], wd_raw.bitcast(U16))
+        wd_sc = sb([P, N], U8, "wd_sc", "wb_sc_raw")
+        deal(wd_sc[:], wd_sc_raw[:])
+
+        tanh, tanh_sq = {}, {}
+
+        def take_tanh(half):
+            tanh[half] = sb([P, PACK, HALF], F32, "tanh%d" % half)
+            for t in range(PACK):
+                nc.scalar.activation(tanh[half][:, t, :], pre[half, t][:], ACT.Tanh, bias=bias[:, t : t + 1])
+
+        def square(q):
+            half, part = divmod(q, 2)
+            tanh_sq[q] = sb([P, QUARTER * PACK], F32, "tanh_sq%d" % q)
+            nc.scalar.activation(
+                tanh_sq[q][:].rearrange("p (c i t) -> p c t i", i=4, t=PACK),
+                tanh[half][:, :, part * QUARTER : (part + 1) * QUARTER].rearrange("p t (c i) -> p c t i", i=4),
+                ACT.Square,
+            )
+
+        h_codes, h_sc = {}, {}
+
+        def make_h(q):
+            neg_h = sb([P, QUARTER * PACK], BF16, "neg_h%d" % q)
+            for b in range(QUARTER // BLOCK):
+                first = q * QUARTER + b * BLOCK
+                half, inside = divmod(first, HALF)
+                err = psum.tile([P, PACK, BLOCK], F32, name="err%d%d" % (q, b), tag="bank%d" % ((2 * q + b) % 3))
+                for t in range(PACK):
+                    for a in range(PASSES):
+                        units = slice(a * H + t * P, a * H + (t + 1) * P)
+                        nc.tensor.matmul_mx(
+                            out=err[:, t, :],
+                            lhsT=wb[:, units].bitcast(FP8X4),
+                            lhsT_scale=wb_sc[:, units],
+                            rhs=v[1, a, half][:, inside : inside + BLOCK].bitcast(FP4X4),
+                            rhs_scale=v_sc[1][a][:, first : first + BLOCK],
+                            start=(a == 0),
+                            stop=(a == PASSES - 1),
+                        )
+                words = slice(b * BLOCK * PACK, (b + 1) * BLOCK * PACK)
+                nc.vector.scalar_tensor_tensor(
+                    out=neg_h[:, words].rearrange("p (j t) -> p j t", t=PACK),
+                    in0=tanh_sq[q][:, words].rearrange("p (j t) -> p j t", t=PACK),
+                    scalar=1.0,
+                    in1=err[:].rearrange("p t j -> p j t"),
+                    op0=ALU.subtract,
+                    op1=ALU.mult,
+                )
+            h_codes[q] = sb([P, QUARTER], U32, "h_codes%d" % q)
+            h_sc[q] = sb([P, QUARTER], U8, "h_sc%d" % q)
+            nc.vector.quantize_mx(out=h_codes[q][:].bitcast(FP8X4), scales=h_sc[q][:], in_=neg_h[:])
+
+        y_rows = out_0.rearrange("(g p t) j -> g p t j", p=P, t=PACK)
+        y_words = out_1.rearrange("g p m t -> p g (m t)").bitcast(I32)
+        y_sc = sb([P, GROUPS * S], U8, "y_sc")
+        y = {}
+
+        def make_y(q):
+            entries = slice(q * QUARTER, (q + 1) * QUARTER)
+            for g in range(GROUPS):
+                y[q, g] = sb([P, PACK, QUARTER], F32, "y%d%d" % (q, g))
+                for pair in range(PACK // 2):
+                    acc = psum.tile([P, 2, QUARTER], F32, name="acc%d%d%d" % (q, g, pair), tag="bank%d" % (3 + (4 * q + 2 * g + pair) % 5))
+                    for u in range(2):
+                        first = g * GROUP + (2 * pair + u) * P
+                        nc.tensor.matmul_mx(
+                            out=acc[:, u, :],
+                            lhsT=wd[:, first : first + P].bitcast(FP4X4),
+                            lhsT_scale=wd_sc[:, first : first + P],
+                            rhs=h_codes[q][:].bitcast(FP8X4),
+                            rhs_scale=h_sc[q][:],
+                            start=True,
+                            stop=True,
+                        )
+                    for u in range(2):
+                        t = 2 * pair + u
+                        nc.scalar.activation(
+                            y[q, g][:, t, :], acc[:, u, :], ACT.Copy,
+                            scale=neg_gain[:, g * PACK + t : g * PACK + t + 1],
+                        )
+                nc.sync.dma_start(y_rows[g][:, :, entries], y[q, g][:])
+
+        def make_planes(q):
+            entries = slice(q * QUARTER, (q + 1) * QUARTER)
+            y_codes = sb([P, GROUPS * QUARTER], U32, "y_codes%d" % q)
+            y_bf = []
+            for g in range(GROUPS):
+                y_bf.append(sb([P, QUARTER * PACK], BF16, "y_bf%d%d" % (q, g)))
+                weave = nc.scalar.copy if (q, g) == (3, 1) else nc.vector.tensor_copy
+                weave(
+                    y_bf[g][:].rearrange("p (c i t) -> p c t i", i=4, t=PACK),
+                    y[q, g][:].rearrange("p t (c i) -> p c t i", i=4),
+                )
+            for g in range(GROUPS):
+                nc.vector.quantize_mx(
+                    out=y_codes[:, g * QUARTER : (g + 1) * QUARTER].bitcast(FP8X4),
+                    scales=y_sc[:, g * S + q * QUARTER : g * S + (q + 1) * QUARTER],
+                    in_=y_bf[g][:],
+                )
+            nc.sync.dma_start(
+                y_words[:, :, entries], y_codes[:].bitcast(I32).rearrange("p (g m) -> p g m", g=GROUPS)
+            )
+
+        take_tanh(0)
+        square(0)
+        take_tanh(1)
+        square(1)
+        square(2)
+        make_h(0)
+        make_y(0)
+        gather(1, 0, 1, "tanh_sq0")
+        gather(1, 1, 1, "neg_h0")
+        square(3)
+        make_h(1)
+        make_y(1)
+        make_h(2)
+        make_planes(0)
+        make_y(2)
+        make_h(3)
+        make_planes(1)
+        make_y(3)
+        make_planes(2)
+        make_planes(3)
+
+        sc_rows = out_2.bitcast(I32).rearrange("g (q r) c -> r q g c", r=4)
+        for r in range(4):
+            queue = nc.sync if r % 2 == 0 else nc.scalar
+            queue.dma_start(
+                sc_rows[r], y_sc[:].bitcast(I32)[r:P:32, :].rearrange("q (g c) -> q g c", g=GROUPS)
+            )

@@ -122,10 +122,10 @@ def tile_list_cocitation_drift_backward_kernel(
             nc.sync.dma_start(moved.bitcast(I32)[0 : P - SHIFT, :], v_sc_lo[:].bitcast(I32)[SHIFT:P, :])
             v_sc.append((v_sc_lo[:], moved))
 
-        def deal(out, in_):
-            nc.vector.tensor_copy(
-                out.rearrange("p (u t m) -> p u m t", t=PACK, m=P),
-                in_.rearrange("p (u m t) -> p u m t", t=PACK, m=P),
+        def deal(out, in_, engine=nc.gpsimd):
+            engine.tensor_copy(
+                out.rearrange("p (u t m) -> p u t m", t=PACK, m=P),
+                in_.rearrange("p (u m t) -> p u t m", t=PACK, m=P),
             )
 
         v = {}
@@ -181,7 +181,7 @@ def tile_list_cocitation_drift_backward_kernel(
         hidden_matmuls(1)
         gather(1, 0, 0, "v010")
         wd = sb([P, N], U16, "wd")
-        deal(wd[:], wd_raw.bitcast(U16))
+        deal(wd[:], wd_raw.bitcast(U16), nc.vector)
         wd_sc = sb([P, N], U8, "wd_sc", "wb_sc_raw")
         deal(wd_sc[:], wd_sc_raw[:])
 

@@ -51,7 +51,10 @@ def tile_list_cocitation_drift_backward_kernel(
         wb_sc_raw = sb([P, PASSES * H], U8, "wb_sc_raw")
         nc.vector.memset(wb_sc_raw[:].bitcast(I32), 0)
 
-        gain_raw = reuse.tile([P, GROUPS, 2 * PACK], F32, name="gain_raw", offset=8160, align_bytes=32)
+        v_sc_hi = sb([P, 2 * S], U8, "v_sc_hi")
+        nc.vector.memset(v_sc_hi[:].bitcast(I32), 0)
+
+        gain_raw = placed([P, GROUPS, 3584], F32, "gain_raw", 0)
         nc.sync.dma_start(gain_raw[:, :, :PACK], gain.rearrange("(g p t) -> p g t", p=P, t=PACK))
         nc.sync.dma_start(idx[0][:], offs)
         nc.sync.dma_start(idx[1][:], offs2)
@@ -102,17 +105,15 @@ def tile_list_cocitation_drift_backward_kernel(
             nc.sync.dma_start(tab[a][:].bitcast(I32), tab_words[a].bitcast(I32))
 
         piece_len = PACK * H // 2
-        w1_first = placed([P, piece_len], F32, "w1_first", 23552)
+        w1_first = placed([P, piece_len], F32, "w1_first", 32768)
         load_w1(0, 0, w1_first[:])
         load_table(0, placed([P, T], U16, "tab0", 0))
-        w1_second = placed([P, piece_len], F32, "w1_second", 8192)
+        w1_second = placed([P, piece_len], F32, "w1_second", 24576)
         load_w1(0, 1, w1_second[:])
-        w1_rest = placed([P, 2 * piece_len], F32, "w1_rest", 16384)
+        w1_rest = placed([P, 2 * piece_len], F32, "w1_rest", 8192)
         for c in range(2):
             load_w1(1, c, w1_rest[:, c * piece_len : (c + 1) * piece_len])
-        load_table(1, placed([P, T], U16, "tab1", 26624))
-        v_sc_hi = placed([P, 2 * S], U8, "v_sc_hi", 24576)
-        nc.vector.memset(v_sc_hi[:].bitcast(I32), 0)
+        load_table(1, placed([P, T], U16, "tab1", 16384))
 
         v_sc = []
         for n in range(2):
@@ -158,30 +159,34 @@ def tile_list_cocitation_drift_backward_kernel(
         for a in range(PASSES):
             quantise_w1(a)
             gather(0, a, 0)
-            gather(0, a, 1)
+            gather(0, a, 1, "w1_bf0" if a == 0 else None)
         gather(1, 1, 0)
 
-        w_raw = placed([P, PASSES * H + N // 2], I32, "w_raw", 9216)
+        w_raw = placed([P, PASSES * H + N // 2], I32, "w_raw", 25600)
         wb_raw = w_raw[:, : PASSES * H]
         wd_raw = w_raw[:, PASSES * H :]
         nc.sync.dma_start(
             wb_raw.rearrange("p (a c) -> p a c", a=PASSES), wb_words.rearrange("a p c i -> p a (c i)").bitcast(I32)
         )
         nc.sync.dma_start(wd_raw, wd_words[0].bitcast(I32))
-        wd_sc_raw = placed([P, N], U8, "wd_sc_raw", 8192)
-        nc.vector.memset(wd_sc_raw[:].bitcast(I32), 0)
+        wd_sc_raw = placed([P, N], U8, "wd_sc_raw", 24576)
+        nc.gpsimd.memset(wd_sc_raw[:].bitcast(I32), 0)
         for r in range(4):
             nc.sync.dma_start(wd_sc_raw[:].bitcast(I32)[r:P:32, :], wd_rows[r])
 
-        wb_sc = sb([P, PASSES * H], U8, "wb_sc", "w1_bf1")
+        wb_sc = sb([P, PASSES * H], U8, "wb_sc")
         deal(wb_sc[:], wb_sc_raw[:])
         wb = sb([P, PASSES * H], I32, "wb")
         deal(wb[:], wb_raw)
         hidden_matmuls(0)
         hidden_matmuls(1)
         gather(1, 0, 0, "v010")
+        gather(1, 0, 1, "v011")
         wd = sb([P, N], U16, "wd")
-        deal(wd[:], wd_raw.bitcast(U16), nc.vector)
+        nc.gpsimd.tensor_copy(
+            wd[:].bitcast(U8).rearrange("p (u t m b) -> p u t m b", t=PACK, m=P, b=2),
+            wd_raw.bitcast(U8).rearrange("p (u m t b) -> p u t m b", t=PACK, m=P, b=2),
+        )
         wd_sc = sb([P, N], U8, "wd_sc", "wb_sc_raw")
         deal(wd_sc[:], wd_sc_raw[:])
 
@@ -232,7 +237,12 @@ def tile_list_cocitation_drift_backward_kernel(
                 )
             h_codes[q] = sb([P, QUARTER], U32, "h_codes%d" % q)
             h_sc[q] = sb([P, QUARTER], U8, "h_sc%d" % q)
-            nc.vector.quantize_mx(out=h_codes[q][:].bitcast(FP8X4), scales=h_sc[q][:], in_=neg_h[:])
+            for b in range(QUARTER // BLOCK):
+                nc.vector.quantize_mx(
+                    out=h_codes[q][:, b * BLOCK : (b + 1) * BLOCK].bitcast(FP8X4),
+                    scales=h_sc[q][:, b * BLOCK : (b + 1) * BLOCK],
+                    in_=neg_h[:, b * BLOCK * PACK : (b + 1) * BLOCK * PACK],
+                )
 
         y_rows = out_0.rearrange("(g p t) j -> g p t j", p=P, t=PACK)
         y_words = out_1.rearrange("g p m t -> p g (m t)").bitcast(I32)
@@ -292,7 +302,6 @@ def tile_list_cocitation_drift_backward_kernel(
         square(2)
         make_h(0)
         make_y(0)
-        gather(1, 0, 1, "tanh_sq0")
         gather(1, 1, 1, "neg_h0")
         square(3)
         make_h(1)

@@ -183,10 +183,7 @@ def tile_list_cocitation_drift_backward_kernel(
         gather(1, 0, 0, "v010")
         gather(1, 0, 1, "v011")
         wd = sb([P, N], U16, "wd")
-        nc.gpsimd.tensor_copy(
-            wd[:].bitcast(U8).rearrange("p (u t m b) -> p u t m b", t=PACK, m=P, b=2),
-            wd_raw.bitcast(U8).rearrange("p (u m t b) -> p u t m b", t=PACK, m=P, b=2),
-        )
+        deal(wd[:], wd_raw.bitcast(U16), nc.vector)
         wd_sc = sb([P, N], U8, "wd_sc", "wb_sc_raw")
         deal(wd_sc[:], wd_sc_raw[:])
 
@@ -268,10 +265,11 @@ def tile_list_cocitation_drift_backward_kernel(
                         )
                     for u in range(2):
                         t = 2 * pair + u
-                        nc.scalar.activation(
-                            y[q, g][:, t, :], acc[:, u, :], ACT.Copy,
-                            scale=neg_gain[:, g * PACK + t : g * PACK + t + 1],
-                        )
+                        factor = neg_gain[:, g * PACK + t : g * PACK + t + 1]
+                        if (q, g) == (3, 1):
+                            nc.vector.tensor_scalar(y[q, g][:, t, :], acc[:, u, :], factor, None, ALU.mult)
+                        else:
+                            nc.scalar.activation(y[q, g][:, t, :], acc[:, u, :], ACT.Copy, scale=factor)
                 nc.sync.dma_start(y_rows[g][:, :, entries], y[q, g][:])
 
         def make_planes(q):
@@ -280,7 +278,7 @@ def tile_list_cocitation_drift_backward_kernel(
             y_bf = []
             for g in range(GROUPS):
                 y_bf.append(sb([P, QUARTER * PACK], BF16, "y_bf%d%d" % (q, g)))
-                weave = nc.scalar.copy if (q, g) == (3, 1) else nc.vector.tensor_copy
+                weave = nc.scalar.copy if [q, g] in [[3,0]] else nc.vector.tensor_copy
                 weave(
                     y_bf[g][:].rearrange("p (c i t) -> p c t i", i=4, t=PACK),
                     y[q, g][:].rearrange("p t (c i) -> p c t i", i=4),

@@ -47,7 +47,8 @@ def tile_list_cocitation_drift_backward_kernel(
         idx = [lists.tile([P, S // 16], U16, name="idx%d" % n) for n in range(2)]
 
         tab_sc = sb([P, T], U8, "tab_sc")
-        nc.vector.memset(tab_sc[:].bitcast(I32), 0)
+        nc.gpsimd.memset(tab_sc[:, : T // 2].bitcast(I32), 0)
+        nc.vector.memset(tab_sc[:, T // 2 :].bitcast(I32), 0)
         wb_sc_raw = sb([P, PASSES * H], U8, "wb_sc_raw")
         nc.vector.memset(wb_sc_raw[:].bitcast(I32), 0)
 
@@ -60,7 +61,8 @@ def tile_list_cocitation_drift_backward_kernel(
         nc.sync.dma_start(idx[1][:], offs2)
         tab_rows = tab_scales.bitcast(I32).rearrange("a (q r) c -> r q a c", r=4)
         for r in range(4):
-            nc.sync.dma_start(tab_sc[:].bitcast(I32)[r:P:SHIFT, :], tab_rows[r])
+            queue = nc.sync if r % 2 == 0 else nc.scalar
+            queue.dma_start(tab_sc[:].bitcast(I32)[r:P:SHIFT, :], tab_rows[r])
 
         bias = sb([P, PACK], F32, "bias")
         nc.gpsimd.dma_start(bias[:], b1.rearrange("(p t) -> p t", t=PACK))
@@ -72,8 +74,8 @@ def tile_list_cocitation_drift_backward_kernel(
             )
 
         neg_gain = sb([P, GROUPS * PACK], F32, "neg_gain")
-        nc.scalar.activation(
-            neg_gain[:].rearrange("p (g t) -> p g t", t=PACK), gain_raw[:, :, :PACK], ACT.Copy, scale=-1.0
+        nc.vector.tensor_scalar(
+            neg_gain[:].rearrange("p (g t) -> p g t", t=PACK), gain_raw[:, :, :PACK], -1.0, None, ALU.mult
         )
 
         w1_rows = w1.rearrange("(a p j) c -> a p j c", p=P, j=PACK)

@@ -49,8 +49,8 @@ def tile_list_cocitation_drift_backward_kernel(
         tab_sc = sb([P, T], U8, "tab_sc")
         nc.gpsimd.memset(tab_sc[:, : T // 2].bitcast(I32), 0)
         nc.vector.memset(tab_sc[:, T // 2 :].bitcast(I32), 0)
-        wb_sc_raw = sb([P, PASSES * H], U8, "wb_sc_raw")
-        nc.vector.memset(wb_sc_raw[:].bitcast(I32), 0)
+        w_sc_raw = sb([P, 2 * N], U8, "w_sc_raw")
+        nc.vector.memset(w_sc_raw[:].bitcast(I32), 0)
 
         v_sc_hi = sb([P, 2 * S], U8, "v_sc_hi")
         nc.vector.memset(v_sc_hi[:].bitcast(I32), 0)
@@ -70,8 +70,10 @@ def tile_list_cocitation_drift_backward_kernel(
         wd_rows = wd_scales[0].bitcast(I32).rearrange("(q r) c -> r q c", r=4)
         for r in range(4):
             nc.gpsimd.dma_start(
-                wb_sc_raw[:].bitcast(I32)[r:P:32, :].rearrange("q (a c) -> q a c", a=PASSES), wb_rows[r]
+                w_sc_raw[:, :N].bitcast(I32)[r:P:32, :].rearrange("q (a c) -> q a c", a=PASSES), wb_rows[r]
             )
+        for r in range(4):
+            nc.gpsimd.dma_start(w_sc_raw[:, N:].bitcast(I32)[r:P:32, :], wd_rows[r])
 
         neg_gain = sb([P, GROUPS * PACK], F32, "neg_gain")
         nc.vector.tensor_scalar(
@@ -80,7 +82,7 @@ def tile_list_cocitation_drift_backward_kernel(
 
         w1_rows = w1.rearrange("(a p j) c -> a p j c", p=P, j=PACK)
         w1_codes, w1_sc = [], []
-        w1_bf = [sb([P, PACK, P, PACK], BF16, "w1_bf0"), sb([P, PACK, P, PACK], BF16, "w1_bf1")]
+        w1_bf = [placed([P, PACK, P, PACK], BF16, "w1_bf%d" % a, 36864 + 4096 * a) for a in range(PASSES)]
 
         def load_w1(a, c, raw):
             piece = raw.rearrange("p (j c) -> p j c", j=PACK)
@@ -161,7 +163,7 @@ def tile_list_cocitation_drift_backward_kernel(
         for a in range(PASSES):
             quantise_w1(a)
             gather(0, a, 0)
-            gather(0, a, 1, "w1_bf0" if a == 0 else None)
+            gather(0, a, 1, offset=36864 if a == 0 else None)
         gather(1, 1, 0)
 
         w_raw = placed([P, PASSES * H + N // 2], I32, "w_raw", 25600)
@@ -171,13 +173,11 @@ def tile_list_cocitation_drift_backward_kernel(
             wb_raw.rearrange("p (a c) -> p a c", a=PASSES), wb_words.rearrange("a p c i -> p a (c i)").bitcast(I32)
         )
         nc.sync.dma_start(wd_raw, wd_words[0].bitcast(I32))
-        wd_sc_raw = placed([P, N], U8, "wd_sc_raw", 24576)
-        nc.gpsimd.memset(wd_sc_raw[:].bitcast(I32), 0)
-        for r in range(4):
-            nc.sync.dma_start(wd_sc_raw[:].bitcast(I32)[r:P:32, :], wd_rows[r])
 
-        wb_sc = sb([P, PASSES * H], U8, "wb_sc")
-        deal(wb_sc[:], wb_sc_raw[:])
+        wb_sc = placed([P, PASSES * H], U8, "wb_sc", 37888)
+        deal(wb_sc[:], w_sc_raw[:, :N])
+        wd_sc = placed([P, N], U8, "wd_sc", 40960)
+        deal(wd_sc[:], w_sc_raw[:, N:])
         wb = sb([P, PASSES * H], I32, "wb")
         deal(wb[:], wb_raw)
         hidden_matmuls(0)
@@ -186,8 +186,6 @@ def tile_list_cocitation_drift_backward_kernel(
         gather(1, 0, 1, "v011")
         wd = sb([P, N], U16, "wd")
         deal(wd[:], wd_raw.bitcast(U16), nc.vector)
-        wd_sc = sb([P, N], U8, "wd_sc", "wb_sc_raw")
-        deal(wd_sc[:], wd_sc_raw[:])
 
         tanh, tanh_sq = {}, {}
 

@@ -47,24 +47,22 @@ def tile_list_cocitation_drift_backward_kernel(
         idx = [lists.tile([P, S // 16], U16, name="idx%d" % n) for n in range(2)]
 
         tab_sc = sb([P, T], U8, "tab_sc")
-        nc.gpsimd.memset(tab_sc[:, : T // 2].bitcast(I32), 0)
-        nc.vector.memset(tab_sc[:, T // 2 :].bitcast(I32), 0)
+        nc.vector.memset(tab_sc[:].bitcast(I32), 0)
         w_sc_raw = sb([P, 2 * N], U8, "w_sc_raw")
         nc.vector.memset(w_sc_raw[:].bitcast(I32), 0)
 
         v_sc_hi = sb([P, 2 * S], U8, "v_sc_hi")
         nc.vector.memset(v_sc_hi[:].bitcast(I32), 0)
 
-        gain_raw = placed([P, GROUPS, 3584], F32, "gain_raw", 0)
+        gain_raw = placed([P, GROUPS, 3976], F32, "gain_raw", 0)
         nc.sync.dma_start(gain_raw[:, :, :PACK], gain.rearrange("(g p t) -> p g t", p=P, t=PACK))
         nc.sync.dma_start(idx[0][:], offs)
         nc.sync.dma_start(idx[1][:], offs2)
         tab_rows = tab_scales.bitcast(I32).rearrange("a (q r) c -> r q a c", r=4)
         for r in range(4):
-            queue = nc.sync if r % 2 == 0 else nc.scalar
-            queue.dma_start(tab_sc[:].bitcast(I32)[r:P:SHIFT, :], tab_rows[r])
+            nc.sync.dma_start(tab_sc[:].bitcast(I32)[r:P:SHIFT, :], tab_rows[r])
 
-        bias = sb([P, PACK], F32, "bias")
+        bias = placed([P, PACK], F32, "bias", 31744)
         nc.gpsimd.dma_start(bias[:], b1.rearrange("(p t) -> p t", t=PACK))
         wb_rows = wb_scales.bitcast(I32).rearrange("a (q r) c -> r q a c", r=4)
         wd_rows = wd_scales[0].bitcast(I32).rearrange("(q r) c -> r q c", r=4)
@@ -76,8 +74,8 @@ def tile_list_cocitation_drift_backward_kernel(
             nc.gpsimd.dma_start(w_sc_raw[:, N:].bitcast(I32)[r:P:32, :], wd_rows[r])
 
         neg_gain = sb([P, GROUPS * PACK], F32, "neg_gain")
-        nc.vector.tensor_scalar(
-            neg_gain[:].rearrange("p (g t) -> p g t", t=PACK), gain_raw[:, :, :PACK], -1.0, None, ALU.mult
+        nc.scalar.activation(
+            neg_gain[:].rearrange("p (g t) -> p g t", t=PACK), gain_raw[:, :, :PACK], ACT.Copy, scale=-1.0
         )
 
         w1_rows = w1.rearrange("(a p j) c -> a p j c", p=P, j=PACK)
@@ -297,13 +295,13 @@ def tile_list_cocitation_drift_backward_kernel(
         square(0)
         take_tanh(1)
         square(1)
-        square(2)
         make_h(0)
         make_y(0)
         gather(1, 1, 1, "neg_h0")
-        square(3)
+        square(2)
         make_h(1)
         make_y(1)
+        square(3)
         make_h(2)
         make_planes(0)
         make_y(2)

@@ -62,8 +62,6 @@ def tile_list_cocitation_drift_backward_kernel(
         for r in range(4):
             nc.sync.dma_start(tab_sc[:].bitcast(I32)[r:P:SHIFT, :], tab_rows[r])
 
-        bias = placed([P, PACK], F32, "bias", 31744)
-        nc.gpsimd.dma_start(bias[:], b1.rearrange("(p t) -> p t", t=PACK))
         wb_rows = wb_scales.bitcast(I32).rearrange("a (q r) c -> r q a c", r=4)
         wd_rows = wd_scales[0].bitcast(I32).rearrange("(q r) c -> r q c", r=4)
         for r in range(4):
@@ -109,6 +107,8 @@ def tile_list_cocitation_drift_backward_kernel(
         piece_len = PACK * H // 2
         w1_first = placed([P, piece_len], F32, "w1_first", 32768)
         load_w1(0, 0, w1_first[:])
+        bias = placed([P, PACK], F32, "bias", 31744)
+        nc.sync.dma_start(bias[:], b1.rearrange("(p t) -> p t", t=PACK))
         load_table(0, placed([P, T], U16, "tab0", 0))
         w1_second = placed([P, piece_len], F32, "w1_second", 24576)
         load_w1(0, 1, w1_second[:])

@@ -80,12 +80,11 @@ def tile_list_cocitation_drift_backward_kernel(
         w1_codes, w1_sc = [], []
         w1_bf = [placed([P, PACK, P, PACK], BF16, "w1_bf%d" % a, 36864 + 4096 * a) for a in range(PASSES)]
 
-        def load_w1(a, c, raw):
-            piece = raw.rearrange("p (j c) -> p j c", j=PACK)
-            nc.sync.dma_start(piece, w1_rows[a][:, :, c * H // 2 : (c + 1) * H // 2])
+        def load_w1(a, raw, rows, columns):
+            nc.sync.dma_start(raw, w1_rows[a][:, rows, columns])
             nc.scalar.activation(
-                w1_bf[a][:, :, c * P // 2 : (c + 1) * P // 2, :].rearrange("p t m j -> p m j t"),
-                piece.rearrange("p j (m t) -> p m j t", t=PACK),
+                w1_bf[a][:, :, columns.start // PACK : columns.stop // PACK, rows].rearrange("p t m j -> p m j t"),
+                raw.rearrange("p j (m t) -> p m j t", t=PACK),
                 ACT.Copy,
             )
 
@@ -104,17 +103,14 @@ def tile_list_cocitation_drift_backward_kernel(
             tab.append(tile)
             nc.sync.dma_start(tab[a][:].bitcast(I32), tab_words[a].bitcast(I32))
 
-        piece_len = PACK * H // 2
-        w1_first = placed([P, piece_len], F32, "w1_first", 32768)
-        load_w1(0, 0, w1_first[:])
+        load_w1(0, placed([P, PACK // 2, H], F32, "w1_first", 32768)[:], slice(0, PACK // 2), slice(0, H))
         bias = placed([P, PACK], F32, "bias", 31744)
         nc.sync.dma_start(bias[:], b1.rearrange("(p t) -> p t", t=PACK))
         load_table(0, placed([P, T], U16, "tab0", 0))
-        w1_second = placed([P, piece_len], F32, "w1_second", 24576)
-        load_w1(0, 1, w1_second[:])
-        w1_rest = placed([P, 2 * piece_len], F32, "w1_rest", 8192)
+        load_w1(0, placed([P, PACK // 2, H], F32, "w1_second", 24576)[:], slice(PACK // 2, PACK), slice(0, H))
+        w1_rest = placed([P, 2, PACK, H // 2], F32, "w1_rest", 8192)
         for c in range(2):
-            load_w1(1, c, w1_rest[:, c * piece_len : (c + 1) * piece_len])
+            load_w1(1, w1_rest[:, c], slice(0, PACK), slice(c * H // 2, (c + 1) * H // 2))
         load_table(1, placed([P, T], U16, "tab1", 16384))
 
         v_sc = []
@@ -158,10 +154,12 @@ def tile_list_cocitation_drift_backward_kernel(
                         stop=(a == PASSES - 1),
                     )
 
-        for a in range(PASSES):
-            quantise_w1(a)
-            gather(0, a, 0)
-            gather(0, a, 1, offset=36864 if a == 0 else None)
+        gather(0, 0, 0)
+        quantise_w1(0)
+        gather(0, 0, 1, offset=36864)
+        quantise_w1(1)
+        gather(0, 1, 0)
+        gather(0, 1, 1)
         gather(1, 1, 0)
 
         w_raw = placed([P, PASSES * H + N // 2], I32, "w_raw", 25600)

@@ -54,7 +54,7 @@ def tile_list_cocitation_drift_backward_kernel(
         v_sc_hi = sb([P, 2 * S], U8, "v_sc_hi")
         nc.vector.memset(v_sc_hi[:].bitcast(I32), 0)
 
-        gain_raw = placed([P, GROUPS, 3976], F32, "gain_raw", 0)
+        gain_raw = placed([P, GROUPS, 4104], F32, "gain_raw", 0)
         nc.sync.dma_start(gain_raw[:, :, :PACK], gain.rearrange("(g p t) -> p g t", p=P, t=PACK))
         nc.sync.dma_start(idx[0][:], offs)
         nc.sync.dma_start(idx[1][:], offs2)
@@ -78,7 +78,7 @@ def tile_list_cocitation_drift_backward_kernel(
 
         w1_rows = w1.rearrange("(a p j) c -> a p j c", p=P, j=PACK)
         w1_codes, w1_sc = [], []
-        w1_bf = [placed([P, PACK, P, PACK], BF16, "w1_bf%d" % a, 36864 + 4096 * a) for a in range(PASSES)]
+        w1_bf = [placed([P, PACK, P, PACK], BF16, "w1_bf%d" % a, 45056 + 4096 * a) for a in range(PASSES)]
 
         def load_w1(a, raw, rows, columns):
             nc.sync.dma_start(raw, w1_rows[a][:, rows, columns])
@@ -103,8 +103,8 @@ def tile_list_cocitation_drift_backward_kernel(
             tab.append(tile)
             nc.sync.dma_start(tab[a][:].bitcast(I32), tab_words[a].bitcast(I32))
 
-        load_w1(0, placed([P, PACK // 2, H], F32, "w1_first", 32768)[:], slice(0, PACK // 2), slice(0, H))
-        bias = placed([P, PACK], F32, "bias", 31744)
+        load_w1(0, placed([P, PACK // 2, H], F32, "w1_first", 40960)[:], slice(0, PACK // 2), slice(0, H))
+        bias = placed([P, PACK], F32, "bias", 29696)
         nc.sync.dma_start(bias[:], b1.rearrange("(p t) -> p t", t=PACK))
         load_table(0, placed([P, T], U16, "tab0", 0))
         load_w1(0, placed([P, PACK // 2, H], F32, "w1_second", 24576)[:], slice(PACK // 2, PACK), slice(0, H))
@@ -112,6 +112,8 @@ def tile_list_cocitation_drift_backward_kernel(
         for c in range(2):
             load_w1(1, w1_rest[:, c], slice(0, PACK), slice(c * H // 2, (c + 1) * H // 2))
         load_table(1, placed([P, T], U16, "tab1", 16384))
+        wd_raw = placed([P, N // 2], I32, "wd_raw", 30720)[:]
+        nc.sync.dma_start(wd_raw, wd_words[0].bitcast(I32))
 
         v_sc = []
         for n in range(2):
@@ -121,8 +123,8 @@ def tile_list_cocitation_drift_backward_kernel(
             nc.sync.dma_start(moved.bitcast(I32)[0 : P - SHIFT, :], v_sc_lo[:].bitcast(I32)[SHIFT:P, :])
             v_sc.append((v_sc_lo[:], moved))
 
-        def deal(out, in_, engine=nc.gpsimd):
-            engine.tensor_copy(
+        def deal(out, in_, copy=nc.gpsimd.tensor_copy):
+            copy(
                 out.rearrange("p (u t m) -> p u t m", t=PACK, m=P),
                 in_.rearrange("p (u m t) -> p u t m", t=PACK, m=P),
             )
@@ -156,23 +158,20 @@ def tile_list_cocitation_drift_backward_kernel(
 
         gather(0, 0, 0)
         quantise_w1(0)
-        gather(0, 0, 1, offset=36864)
+        gather(0, 0, 1, offset=45056)
         quantise_w1(1)
         gather(0, 1, 0)
         gather(0, 1, 1)
         gather(1, 1, 0)
 
-        w_raw = placed([P, PASSES * H + N // 2], I32, "w_raw", 25600)
-        wb_raw = w_raw[:, : PASSES * H]
-        wd_raw = w_raw[:, PASSES * H :]
+        wb_raw = placed([P, PASSES * H], I32, "wb_raw", 25600)[:]
         nc.sync.dma_start(
             wb_raw.rearrange("p (a c) -> p a c", a=PASSES), wb_words.rearrange("a p c i -> p a (c i)").bitcast(I32)
         )
-        nc.sync.dma_start(wd_raw, wd_words[0].bitcast(I32))
 
-        wb_sc = placed([P, PASSES * H], U8, "wb_sc", 37888)
+        wb_sc = placed([P, PASSES * H], U8, "wb_sc", 46080)
         deal(wb_sc[:], w_sc_raw[:, :N])
-        wd_sc = placed([P, N], U8, "wd_sc", 40960)
+        wd_sc = placed([P, N], U8, "wd_sc", 49152)
         deal(wd_sc[:], w_sc_raw[:, N:])
         wb = sb([P, PASSES * H], I32, "wb")
         deal(wb[:], wb_raw)
@@ -181,18 +180,30 @@ def tile_list_cocitation_drift_backward_kernel(
         gather(1, 0, 0, "v010")
         gather(1, 0, 1, "v011")
         wd = sb([P, N], U16, "wd")
-        deal(wd[:], wd_raw.bitcast(U16), nc.vector)
+        deal(wd[:], wd_raw.bitcast(U16), nc.scalar.copy)
 
         tanh, tanh_sq = {}, {}
 
         def take_tanh(half):
-            tanh[half] = sb([P, PACK, HALF], F32, "tanh%d" % half)
+            if half == 0:
+                tanh[half] = placed([P, PACK, HALF], F32, "tanh0", 32704)
+            else:
+                tanh[half] = sb([P, PACK, HALF], F32, "tanh1")
             for t in range(PACK):
                 nc.scalar.activation(tanh[half][:, t, :], pre[half, t][:], ACT.Tanh, bias=bias[:, t : t + 1])
 
-        def square(q):
+        def square_on_gpsimd(q):
             half, part = divmod(q, 2)
             tanh_sq[q] = sb([P, QUARTER * PACK], F32, "tanh_sq%d" % q)
+            for b in range(QUARTER // BLOCK):
+                first = part * QUARTER + b * BLOCK
+                rows = tanh[half][:, :, first : first + BLOCK].rearrange("p t j -> p j t")
+                words = tanh_sq[q][:, b * BLOCK * PACK : (b + 1) * BLOCK * PACK]
+                nc.gpsimd.tensor_tensor(words.rearrange("p (j t) -> p j t", t=PACK), rows, rows, ALU.mult)
+
+        def square(q, tag=None):
+            half, part = divmod(q, 2)
+            tanh_sq[q] = sb([P, QUARTER * PACK], F32, "tanh_sq%d" % q, tag)
             nc.scalar.activation(
                 tanh_sq[q][:].rearrange("p (c i t) -> p c t i", i=4, t=PACK),
                 tanh[half][:, :, part * QUARTER : (part + 1) * QUARTER].rearrange("p t (c i) -> p c t i", i=4),
@@ -201,12 +212,12 @@ def tile_list_cocitation_drift_backward_kernel(
 
         h_codes, h_sc = {}, {}
 
-        def make_h(q):
+        def make_h(q, banks):
             neg_h = sb([P, QUARTER * PACK], BF16, "neg_h%d" % q)
             for b in range(QUARTER // BLOCK):
                 first = q * QUARTER + b * BLOCK
                 half, inside = divmod(first, HALF)
-                err = psum.tile([P, PACK, BLOCK], F32, name="err%d%d" % (q, b), tag="bank%d" % ((2 * q + b) % 3))
+                err = psum.tile([P, PACK, BLOCK], F32, name="err%d%d" % (q, b), tag="bank%d" % banks[b])
                 for t in range(PACK):
                     for a in range(PASSES):
                         units = slice(a * H + t * P, a * H + (t + 1) * P)
@@ -242,12 +253,12 @@ def tile_list_cocitation_drift_backward_kernel(
         y_sc = sb([P, GROUPS * S], U8, "y_sc")
         y = {}
 
-        def make_y(q):
+        def make_y(q, groups, banks):
             entries = slice(q * QUARTER, (q + 1) * QUARTER)
-            for g in range(GROUPS):
+            for g in groups:
                 y[q, g] = sb([P, PACK, QUARTER], F32, "y%d%d" % (q, g))
                 for pair in range(PACK // 2):
-                    acc = psum.tile([P, 2, QUARTER], F32, name="acc%d%d%d" % (q, g, pair), tag="bank%d" % (3 + (4 * q + 2 * g + pair) % 5))
+                    acc = psum.tile([P, 2, QUARTER], F32, name="acc%d%d%d" % (q, g, pair), tag="bank%d" % banks[pair])
                     for u in range(2):
                         first = g * GROUP + (2 * pair + u) * P
                         nc.tensor.matmul_mx(
@@ -262,20 +273,16 @@ def tile_list_cocitation_drift_backward_kernel(
                     for u in range(2):
                         t = 2 * pair + u
                         factor = neg_gain[:, g * PACK + t : g * PACK + t + 1]
-                        if (q, g) == (3, 1):
-                            nc.vector.tensor_scalar(y[q, g][:, t, :], acc[:, u, :], factor, None, ALU.mult)
-                        else:
-                            nc.scalar.activation(y[q, g][:, t, :], acc[:, u, :], ACT.Copy, scale=factor)
+                        nc.scalar.activation(y[q, g][:, t, :], acc[:, u, :], ACT.Copy, scale=factor)
                 nc.sync.dma_start(y_rows[g][:, :, entries], y[q, g][:])
 
-        def make_planes(q):
+        def make_planes(q, tags=(None, None)):
             entries = slice(q * QUARTER, (q + 1) * QUARTER)
             y_codes = sb([P, GROUPS * QUARTER], U32, "y_codes%d" % q)
             y_bf = []
             for g in range(GROUPS):
-                y_bf.append(sb([P, QUARTER * PACK], BF16, "y_bf%d%d" % (q, g)))
-                weave = nc.scalar.copy if [q, g] in [[3,0]] else nc.vector.tensor_copy
-                weave(
+                y_bf.append(sb([P, QUARTER * PACK], BF16, "y_bf%d%d" % (q, g), tags[g]))
+                nc.vector.tensor_copy(
                     y_bf[g][:].rearrange("p (c i t) -> p c t i", i=4, t=PACK),
                     y[q, g][:].rearrange("p t (c i) -> p c t i", i=4),
                 )
@@ -291,21 +298,25 @@ def tile_list_cocitation_drift_backward_kernel(
 
         take_tanh(0)
         square(0)
+        square_on_gpsimd(1)
         take_tanh(1)
-        square(1)
-        make_h(0)
-        make_y(0)
+        make_h(0, (0, 1))
+        make_y(0, (0,), (4, 5))
+        make_y(0, (1,), (6, 7))
         gather(1, 1, 1, "neg_h0")
-        square(2)
-        make_h(1)
-        make_y(1)
-        square(3)
-        make_h(2)
-        make_planes(0)
-        make_y(2)
-        make_h(3)
+        make_h(1, (2, 3))
+        square(2, "h_codes0")
+        make_y(1, (0,), (0, 1))
+        make_planes(0, ("tanh_sq1", "neg_h1"))
+        make_h(2, (2, 3))
+        square(3, "h_sc1")
+        make_y(1, (1,), (4, 5))
+        make_h(3, (2, 3))
+        make_y(2, (0,), (6, 7))
+        make_y(2, (1,), (0, 1))
         make_planes(1)
-        make_y(3)
+        make_y(3, (0,), (4, 5))
+        make_y(3, (1,), (6, 7))
         make_planes(2)
         make_planes(3)
 

@@ -139,46 +139,45 @@ def tile_list_cocitation_drift_backward_kernel(
 
         pre = {}
 
-        def hidden_matmuls(half):
+        def hidden_matmuls(half, order):
             entries = slice(half * HALF, (half + 1) * HALF)
             for t in range(PACK):
-                pre[half, t] = psum.tile([P, HALF], F32, name="pre%d%d" % (half, t), tag="bank%d" % (half * PACK + t))
-            for a in range(PASSES):
-                for t in range(PACK):
-                    units = slice(t * P, (t + 1) * P)
-                    nc.tensor.matmul_mx(
-                        out=pre[half, t][:],
-                        lhsT=w1_codes[a][:, units].bitcast(FP8X4),
-                        lhsT_scale=w1_sc[a][:, units],
-                        rhs=v[0, a, half][:].bitcast(FP4X4),
-                        rhs_scale=v_sc[0][a][:, entries],
-                        start=(a == 0),
-                        stop=(a == PASSES - 1),
-                    )
+                pre[half, t] = psum.tile([P, HALF], F32, name="pre%d%d" % (half, t), tag="bank%d" % t)
+            for a, t in order:
+                units = slice(t * P, (t + 1) * P)
+                nc.tensor.matmul_mx(
+                    out=pre[half, t][:],
+                    lhsT=w1_codes[a][:, units].bitcast(FP8X4),
+                    lhsT_scale=w1_sc[a][:, units],
+                    rhs=v[0, a, half][:].bitcast(FP4X4),
+                    rhs_scale=v_sc[0][a][:, entries],
+                    start=(a == 0),
+                    stop=(a == PASSES - 1),
+                )
 
         gather(0, 0, 0)
         quantise_w1(0)
         gather(0, 0, 1, offset=45056)
         quantise_w1(1)
-        gather(0, 1, 0)
+        gather(0, 1, 0, offset=57344)
         gather(0, 1, 1)
         gather(1, 1, 0)
 
-        wb_raw = placed([P, PASSES * H], I32, "wb_raw", 25600)[:]
-        nc.sync.dma_start(
-            wb_raw.rearrange("p (a c) -> p a c", a=PASSES), wb_words.rearrange("a p c i -> p a (c i)").bitcast(I32)
-        )
-
-        wb_sc = placed([P, PASSES * H], U8, "wb_sc", 46080)
+        wb_sc = sb([P, PASSES * H], U8, "wb_sc")
         deal(wb_sc[:], w_sc_raw[:, :N])
-        wd_sc = placed([P, N], U8, "wd_sc", 49152)
-        deal(wd_sc[:], w_sc_raw[:, N:])
-        wb = sb([P, PASSES * H], I32, "wb")
-        deal(wb[:], wb_raw)
-        hidden_matmuls(0)
-        hidden_matmuls(1)
-        gather(1, 0, 0, "v010")
-        gather(1, 0, 1, "v011")
+        wd_sc = []
+        for g in range(GROUPS):
+            wd_sc.append(placed([P, GROUP], U8, "wd_sc%d" % g, 46080 + 4096 * g))
+            deal(wd_sc[g][:], w_sc_raw[:, N + g * GROUP : N + (g + 1) * GROUP])
+        wb = []
+        for a in range(PASSES):
+            wb_raw = placed([P, H], I32, "wb_raw%d" % a, 24576 + 2048 * a)
+            nc.sync.dma_start(wb_raw[:], wb_words[a].rearrange("p c i -> p (c i)").bitcast(I32))
+            wb.append(sb([P, H], I32, "wb%d" % a))
+            deal(wb[a][:], wb_raw[:])
+        hidden_matmuls(0, [(a, t) for a in range(PASSES) for t in range(PACK)])
+        gather(1, 0, 0, offset=57344 - 960)
+        gather(1, 0, 1, offset=57344 + 960)
         wd = sb([P, N], U16, "wd")
         deal(wd[:], wd_raw.bitcast(U16), nc.scalar.copy)
 
@@ -192,14 +191,14 @@ def tile_list_cocitation_drift_backward_kernel(
             for t in range(PACK):
                 nc.scalar.activation(tanh[half][:, t, :], pre[half, t][:], ACT.Tanh, bias=bias[:, t : t + 1])
 
-        def square_on_gpsimd(q):
+        squares = {}
+
+        def square_on_gpsimd(q, b, tile):
             half, part = divmod(q, 2)
-            tanh_sq[q] = sb([P, QUARTER * PACK], F32, "tanh_sq%d" % q)
-            for b in range(QUARTER // BLOCK):
-                first = part * QUARTER + b * BLOCK
-                rows = tanh[half][:, :, first : first + BLOCK].rearrange("p t j -> p j t")
-                words = tanh_sq[q][:, b * BLOCK * PACK : (b + 1) * BLOCK * PACK]
-                nc.gpsimd.tensor_tensor(words.rearrange("p (j t) -> p j t", t=PACK), rows, rows, ALU.mult)
+            first = part * QUARTER + b * BLOCK
+            rows = tanh[half][:, :, first : first + BLOCK].rearrange("p t j -> p j t")
+            squares[q, b] = tile[:]
+            nc.gpsimd.tensor_tensor(tile[:], rows, rows, ALU.mult)
 
         def square(q, tag=None):
             half, part = divmod(q, 2)
@@ -209,31 +208,35 @@ def tile_list_cocitation_drift_backward_kernel(
                 tanh[half][:, :, part * QUARTER : (part + 1) * QUARTER].rearrange("p t (c i) -> p c t i", i=4),
                 ACT.Square,
             )
+            for b in range(QUARTER // BLOCK):
+                words = tanh_sq[q][:, b * BLOCK * PACK : (b + 1) * BLOCK * PACK]
+                squares[q, b] = words.rearrange("p (j t) -> p j t", t=PACK)
 
         h_codes, h_sc = {}, {}
 
-        def make_h(q, banks):
-            neg_h = sb([P, QUARTER * PACK], BF16, "neg_h%d" % q)
+        def make_h(q, banks, neg_h=None, passes=(0, 1)):
+            if neg_h is None:
+                neg_h = sb([P, QUARTER * PACK], BF16, "neg_h%d" % q)
             for b in range(QUARTER // BLOCK):
                 first = q * QUARTER + b * BLOCK
                 half, inside = divmod(first, HALF)
                 err = psum.tile([P, PACK, BLOCK], F32, name="err%d%d" % (q, b), tag="bank%d" % banks[b])
-                for t in range(PACK):
-                    for a in range(PASSES):
+                for a in passes:
+                    for t in range(PACK):
                         units = slice(a * H + t * P, a * H + (t + 1) * P)
                         nc.tensor.matmul_mx(
                             out=err[:, t, :],
-                            lhsT=wb[:, units].bitcast(FP8X4),
+                            lhsT=wb[a][:, t * P : (t + 1) * P].bitcast(FP8X4),
                             lhsT_scale=wb_sc[:, units],
                             rhs=v[1, a, half][:, inside : inside + BLOCK].bitcast(FP4X4),
                             rhs_scale=v_sc[1][a][:, first : first + BLOCK],
-                            start=(a == 0),
-                            stop=(a == PASSES - 1),
+                            start=(a == passes[0] and t == 0),
+                            stop=(a == passes[-1] and t == PACK - 1),
                         )
                 words = slice(b * BLOCK * PACK, (b + 1) * BLOCK * PACK)
                 nc.vector.scalar_tensor_tensor(
                     out=neg_h[:, words].rearrange("p (j t) -> p j t", t=PACK),
-                    in0=tanh_sq[q][:, words].rearrange("p (j t) -> p j t", t=PACK),
+                    in0=squares[q, b],
                     scalar=1.0,
                     in1=err[:].rearrange("p t j -> p j t"),
                     op0=ALU.subtract,
@@ -264,7 +267,7 @@ def tile_list_cocitation_drift_backward_kernel(
                         nc.tensor.matmul_mx(
                             out=acc[:, u, :],
                             lhsT=wd[:, first : first + P].bitcast(FP4X4),
-                            lhsT_scale=wd_sc[:, first : first + P],
+                            lhsT_scale=wd_sc[g][:, first - g * GROUP : first - g * GROUP + P],
                             rhs=h_codes[q][:].bitcast(FP8X4),
                             rhs_scale=h_sc[q][:],
                             start=True,
@@ -276,12 +279,11 @@ def tile_list_cocitation_drift_backward_kernel(
                         nc.scalar.activation(y[q, g][:, t, :], acc[:, u, :], ACT.Copy, scale=factor)
                 nc.sync.dma_start(y_rows[g][:, :, entries], y[q, g][:])
 
-        def make_planes(q, tags=(None, None)):
+        def make_planes(q, y_bf=None):
             entries = slice(q * QUARTER, (q + 1) * QUARTER)
             y_codes = sb([P, GROUPS * QUARTER], U32, "y_codes%d" % q)
-            y_bf = []
+            y_bf = y_bf or [sb([P, QUARTER * PACK], BF16, "y_bf%d%d" % (q, g)) for g in range(GROUPS)]
             for g in range(GROUPS):
-                y_bf.append(sb([P, QUARTER * PACK], BF16, "y_bf%d%d" % (q, g), tags[g]))
                 nc.vector.tensor_copy(
                     y_bf[g][:].rearrange("p (c i t) -> p c t i", i=4, t=PACK),
                     y[q, g][:].rearrange("p t (c i) -> p c t i", i=4),
@@ -298,25 +300,27 @@ def tile_list_cocitation_drift_backward_kernel(
 
         take_tanh(0)
         square(0)
-        square_on_gpsimd(1)
+        square_on_gpsimd(1, 0, placed([P, BLOCK, PACK], F32, "tanh_sq10", 26624))
+        hidden_matmuls(1, [(a, t) for t in range(PACK) for a in range(PASSES)])
         take_tanh(1)
-        make_h(0, (0, 1))
+        make_h(0, (4, 5), placed([P, QUARTER * PACK], BF16, "neg_h0", 53248), passes=(1, 0))
+        square_on_gpsimd(1, 1, placed([P, BLOCK, PACK], F32, "tanh_sq11", 54272))
         make_y(0, (0,), (4, 5))
-        make_y(0, (1,), (6, 7))
-        gather(1, 1, 1, "neg_h0")
-        make_h(1, (2, 3))
+        make_y(0, (1,), (0, 1))
+        gather(1, 1, 1, offset=53248)
+        make_h(1, (6, 7), passes=(1, 0))
         square(2, "h_codes0")
-        make_y(1, (0,), (0, 1))
-        make_planes(0, ("tanh_sq1", "neg_h1"))
-        make_h(2, (2, 3))
+        make_y(1, (0,), (2, 3))
+        make_planes(0, [placed([P, QUARTER * PACK], BF16, "y_bf00", 54272), sb([P, QUARTER * PACK], BF16, "y_bf01", "neg_h1")])
+        make_h(2, (6, 7))
         square(3, "h_sc1")
         make_y(1, (1,), (4, 5))
-        make_h(3, (2, 3))
-        make_y(2, (0,), (6, 7))
-        make_y(2, (1,), (0, 1))
+        make_h(3, (6, 7))
+        make_y(2, (0,), (0, 1))
+        make_y(2, (1,), (2, 3))
         make_planes(1)
         make_y(3, (0,), (4, 5))
-        make_y(3, (1,), (6, 7))
+        make_y(3, (1,), (0, 1))
         make_planes(2)
         make_planes(3)
 

@@ -181,7 +181,7 @@ def tile_list_cocitation_drift_backward_kernel(
         wd = sb([P, N], U16, "wd")
         deal(wd[:], wd_raw.bitcast(U16), nc.scalar.copy)
 
-        tanh, tanh_sq = {}, {}
+        tanh = {}
 
         def take_tanh(half):
             if half == 0:
@@ -200,16 +200,17 @@ def tile_list_cocitation_drift_backward_kernel(
             squares[q, b] = tile[:]
             nc.gpsimd.tensor_tensor(tile[:], rows, rows, ALU.mult)
 
-        def square(q, tag=None):
+        def square(q, blocks, tag=None):
             half, part = divmod(q, 2)
-            tanh_sq[q] = sb([P, QUARTER * PACK], F32, "tanh_sq%d" % q, tag)
+            first = part * QUARTER + blocks[0] * BLOCK
+            tile = sb([P, len(blocks) * BLOCK * PACK], F32, "tanh_sq%d%d" % (q, blocks[0]), tag)
             nc.scalar.activation(
-                tanh_sq[q][:].rearrange("p (c i t) -> p c t i", i=4, t=PACK),
-                tanh[half][:, :, part * QUARTER : (part + 1) * QUARTER].rearrange("p t (c i) -> p c t i", i=4),
+                tile[:].rearrange("p (c i t) -> p c t i", i=4, t=PACK),
+                tanh[half][:, :, first : first + len(blocks) * BLOCK].rearrange("p t (c i) -> p c t i", i=4),
                 ACT.Square,
             )
-            for b in range(QUARTER // BLOCK):
-                words = tanh_sq[q][:, b * BLOCK * PACK : (b + 1) * BLOCK * PACK]
+            for n, b in enumerate(blocks):
+                words = tile[:, n * BLOCK * PACK : (n + 1) * BLOCK * PACK]
                 squares[q, b] = words.rearrange("p (j t) -> p j t", t=PACK)
 
         h_codes, h_sc = {}, {}
@@ -279,15 +280,19 @@ def tile_list_cocitation_drift_backward_kernel(
                         nc.scalar.activation(y[q, g][:, t, :], acc[:, u, :], ACT.Copy, scale=factor)
                 nc.sync.dma_start(y_rows[g][:, :, entries], y[q, g][:])
 
-        def make_planes(q, y_bf=None):
+        def make_planes(q, y_bf=None, shared=()):
             entries = slice(q * QUARTER, (q + 1) * QUARTER)
             y_codes = sb([P, GROUPS * QUARTER], U32, "y_codes%d" % q)
             y_bf = y_bf or [sb([P, QUARTER * PACK], BF16, "y_bf%d%d" % (q, g)) for g in range(GROUPS)]
             for g in range(GROUPS):
-                nc.vector.tensor_copy(
-                    y_bf[g][:].rearrange("p (c i t) -> p c t i", i=4, t=PACK),
-                    y[q, g][:].rearrange("p t (c i) -> p c t i", i=4),
-                )
+                copies = (nc.vector.tensor_copy, nc.scalar.copy) if g in shared else (nc.vector.tensor_copy,)
+                width = QUARTER // len(copies)
+                for n, copy in enumerate(copies):
+                    words = y_bf[g][:, n * width * PACK : (n + 1) * width * PACK]
+                    copy(
+                        words.rearrange("p (c i t) -> p c t i", i=4, t=PACK),
+                        y[q, g][:, :, n * width : (n + 1) * width].rearrange("p t (c i) -> p c t i", i=4),
+                    )
             for g in range(GROUPS):
                 nc.vector.quantize_mx(
                     out=y_codes[:, g * QUARTER : (g + 1) * QUARTER].bitcast(FP8X4),
@@ -299,21 +304,22 @@ def tile_list_cocitation_drift_backward_kernel(
             )
 
         take_tanh(0)
-        square(0)
+        square(0, (0, 1))
         square_on_gpsimd(1, 0, placed([P, BLOCK, PACK], F32, "tanh_sq10", 26624))
         hidden_matmuls(1, [(a, t) for t in range(PACK) for a in range(PASSES)])
         take_tanh(1)
+        square(2, (0,))
         make_h(0, (4, 5), placed([P, QUARTER * PACK], BF16, "neg_h0", 53248), passes=(1, 0))
         square_on_gpsimd(1, 1, placed([P, BLOCK, PACK], F32, "tanh_sq11", 54272))
         make_y(0, (0,), (4, 5))
         make_y(0, (1,), (0, 1))
         gather(1, 1, 1, offset=53248)
         make_h(1, (6, 7), passes=(1, 0))
-        square(2, "h_codes0")
+        square(2, (1,), "h_codes0")
         make_y(1, (0,), (2, 3))
         make_planes(0, [placed([P, QUARTER * PACK], BF16, "y_bf00", 54272), sb([P, QUARTER * PACK], BF16, "y_bf01", "neg_h1")])
         make_h(2, (6, 7))
-        square(3, "h_sc1")
+        square(3, (0, 1), "h_sc1")
         make_y(1, (1,), (4, 5))
         make_h(3, (6, 7))
         make_y(2, (0,), (0, 1))
@@ -322,7 +328,7 @@ def tile_list_cocitation_drift_backward_kernel(
         make_y(3, (0,), (4, 5))
         make_y(3, (1,), (0, 1))
         make_planes(2)
-        make_planes(3)
+        make_planes(3, shared=(1,))
 
         sc_rows = out_2.bitcast(I32).rearrange("g (q r) c -> r q g c", r=4)
         for r in range(4):

@@ -25,6 +25,78 @@ HALF = S // 2
 QUARTER = S // 4
 BLOCK = 128
 SHIFT = 16
+ALIGN = 64
+
+TILES = {
+    "tab_sc": (U8, 1, [T]),
+    "w_sc_raw": (U8, 1, [2 * N]),
+    "v_sc_hi": (U8, 1, [2 * S]),
+    "gain_raw": (F32, 4, [GROUPS, PACK]),
+    "neg_gain": (F32, 4, [GROUPS * PACK]),
+    "bias": (F32, 4, [PACK]),
+    "w1_first": (F32, 4, [PACK // 2, H]),
+    "w1_second": (F32, 4, [PACK // 2, H]),
+    "w1_third": (F32, 4, [PACK, H // 2]),
+    "w1_fourth": (F32, 4, [PACK, H // 2]),
+    "wd_raw": (I32, 4, [N // 2]),
+    "wd": (U16, 2, [N]),
+    "wb_sc": (U8, 1, [PASSES * H]),
+    "y_sc": (U8, 1, [GROUPS * S]),
+    **{"tab%d" % a: (U16, 2, [T]) for a in range(PASSES)},
+    **{"w1_bf%d" % a: (BF16, 2, [PACK, P, PACK]) for a in range(PASSES)},
+    **{"w1_codes%d" % a: (U32, 4, [H]) for a in range(PASSES)},
+    **{"w1_sc%d" % a: (U8, 1, [H]) for a in range(PASSES)},
+    **{"wb_raw%d" % a: (I32, 4, [H]) for a in range(PASSES)},
+    **{"wb%d" % a: (I32, 4, [H]) for a in range(PASSES)},
+    **{"wd_sc%d" % g: (U8, 1, [GROUP]) for g in range(GROUPS)},
+    **{"v_sc_lo%d" % n: (U8, 1, [S]) for n in range(2)},
+    **{"v%d%d%d" % (n, a, h): (U16, 2, [HALF]) for n in range(2) for a in range(PASSES) for h in range(2)},
+    **{"tanh%d" % h: (F32, 4, [PACK, HALF]) for h in range(2)},
+    **{"sq%d%d" % (q, b): (F32, 4, [BLOCK, PACK]) for q in range(4) for b in range(2)},
+    **{"neg_h%d" % q: (BF16, 2, [QUARTER * PACK]) for q in range(4)},
+    **{"h_codes%d" % q: (U32, 4, [QUARTER]) for q in range(4)},
+    **{"h_sc%d" % q: (U8, 1, [QUARTER]) for q in range(4)},
+    **{"y%d%d" % (q, g): (F32, 4, [PACK, QUARTER]) for q in range(4) for g in range(GROUPS)},
+    **{"y_bf%d%d" % (q, g): (BF16, 2, [QUARTER * PACK]) for q in range(4) for g in range(GROUPS)},
+    **{"y_codes%d" % q: (U32, 4, [GROUPS * QUARTER]) for q in range(4)},
+}
+
+HEIRS = {
+    "gain_raw": ["bias", "w1_second", "tab0", "w1_third", "w1_fourth", "tab1", "wd_raw"],
+    "w1_second": ["v001", "wb_raw0", "wb_raw1"],
+    "wb_raw1": ["sq10"],
+    "wd_raw": ["tanh0"],
+    "w1_bf0": ["wd_sc0"],
+    "w1_bf1": ["wd_sc1"],
+    "v010": ["v100", "v101"],
+    "sq01": ["v111"],
+    "neg_h0": ["sq11"],
+    "sq11": ["y_bf00"],
+    "neg_h1": ["y_bf01"],
+    "h_codes0": ["sq21"],
+    "h_sc1": ["sq30", "sq31"],
+}
+
+
+def elements(name):
+    count = 1
+    for size in TILES[name][2]:
+        count = count * size
+    return count
+
+
+def span(name):
+    own = -(-elements(name) * TILES[name][1] // ALIGN) * ALIGN
+    return max(own, sum(span(heir) for heir in HEIRS.get(name, [])))
+
+
+def lay_out(names, start):
+    places = {}
+    for name in names:
+        places[name] = start
+        places.update(lay_out(HEIRS.get(name, []), start))
+        start = start + span(name)
+    return places
 
 
 def tile_list_cocitation_drift_backward_kernel(
@@ -32,96 +104,89 @@ def tile_list_cocitation_drift_backward_kernel(
     out_0, out_1, out_2,
 ):
     nc = tc.nc
+    heirs = [heir for names in HEIRS.values() for heir in names]
+    places = lay_out([name for name in TILES if name not in heirs], 0)
     with ExitStack() as ctx:
         lists = ctx.enter_context(tc.tile_pool(name="lists", bufs=1))
         pool = ctx.enter_context(tc.tile_pool(name="pool", bufs=1))
-        reuse = ctx.enter_context(tc.tile_pool(name="reuse", bufs=1))
         psum = ctx.enter_context(tc.psum_pool(name="psum", bufs=1))
+        made = {}
 
-        def sb(shape, dtype, name, tag=None):
-            return pool.tile(shape, dtype, name=name, tag=tag or name, align_bytes=64)
-
-        def placed(shape, dtype, name, offset):
-            return reuse.tile(shape, dtype, name=name, offset=offset, align_bytes=64)
+        def sb(name):
+            if name not in made:
+                dtype, width, shape = TILES[name]
+                tile = pool.tile([P, span(name) // width], dtype, name=name, offset=places[name], align_bytes=ALIGN)
+                view = tile[:, : elements(name)]
+                if len(shape) == 2:
+                    view = view.rearrange("p (a b) -> p a b", a=shape[0])
+                if len(shape) == 3:
+                    view = view.rearrange("p (a b c) -> p a b c", a=shape[0], b=shape[1])
+                made[name] = view
+            return made[name]
 
         idx = [lists.tile([P, S // 16], U16, name="idx%d" % n) for n in range(2)]
 
-        tab_sc = sb([P, T], U8, "tab_sc")
-        nc.vector.memset(tab_sc[:].bitcast(I32), 0)
-        w_sc_raw = sb([P, 2 * N], U8, "w_sc_raw")
-        nc.vector.memset(w_sc_raw[:].bitcast(I32), 0)
+        for name in ("tab_sc", "w_sc_raw", "v_sc_hi"):
+            nc.vector.memset(sb(name).bitcast(I32), 0)
 
-        v_sc_hi = sb([P, 2 * S], U8, "v_sc_hi")
-        nc.vector.memset(v_sc_hi[:].bitcast(I32), 0)
-
-        gain_raw = placed([P, GROUPS, 4104], F32, "gain_raw", 0)
-        nc.sync.dma_start(gain_raw[:, :, :PACK], gain.rearrange("(g p t) -> p g t", p=P, t=PACK))
+        nc.sync.dma_start(sb("gain_raw"), gain.rearrange("(g p t) -> p g t", p=P, t=PACK))
         nc.sync.dma_start(idx[0][:], offs)
         nc.sync.dma_start(idx[1][:], offs2)
         tab_rows = tab_scales.bitcast(I32).rearrange("a (q r) c -> r q a c", r=4)
         for r in range(4):
-            nc.sync.dma_start(tab_sc[:].bitcast(I32)[r:P:SHIFT, :], tab_rows[r])
+            nc.sync.dma_start(sb("tab_sc").bitcast(I32)[r:P:SHIFT, :], tab_rows[r])
 
         wb_rows = wb_scales.bitcast(I32).rearrange("a (q r) c -> r q a c", r=4)
         wd_rows = wd_scales[0].bitcast(I32).rearrange("(q r) c -> r q c", r=4)
         for r in range(4):
             nc.gpsimd.dma_start(
-                w_sc_raw[:, :N].bitcast(I32)[r:P:32, :].rearrange("q (a c) -> q a c", a=PASSES), wb_rows[r]
+                sb("w_sc_raw")[:, :N].bitcast(I32)[r:P:32, :].rearrange("q (a c) -> q a c", a=PASSES), wb_rows[r]
             )
         for r in range(4):
-            nc.gpsimd.dma_start(w_sc_raw[:, N:].bitcast(I32)[r:P:32, :], wd_rows[r])
+            nc.gpsimd.dma_start(sb("w_sc_raw")[:, N:].bitcast(I32)[r:P:32, :], wd_rows[r])
 
-        neg_gain = sb([P, GROUPS * PACK], F32, "neg_gain")
         nc.scalar.activation(
-            neg_gain[:].rearrange("p (g t) -> p g t", t=PACK), gain_raw[:, :, :PACK], ACT.Copy, scale=-1.0
+            sb("neg_gain").rearrange("p (g t) -> p g t", t=PACK), sb("gain_raw"), ACT.Copy, scale=-1.0
         )
 
         w1_rows = w1.rearrange("(a p j) c -> a p j c", p=P, j=PACK)
-        w1_codes, w1_sc = [], []
-        w1_bf = [placed([P, PACK, P, PACK], BF16, "w1_bf%d" % a, 45056 + 4096 * a) for a in range(PASSES)]
 
-        def load_w1(a, raw, rows, columns):
-            nc.sync.dma_start(raw, w1_rows[a][:, rows, columns])
+        def load_w1(a, name, rows, columns):
+            nc.sync.dma_start(sb(name), w1_rows[a][:, rows, columns])
             nc.scalar.activation(
-                w1_bf[a][:, :, columns.start // PACK : columns.stop // PACK, rows].rearrange("p t m j -> p m j t"),
-                raw.rearrange("p j (m t) -> p m j t", t=PACK),
+                sb("w1_bf%d" % a)[:, :, columns.start // PACK : columns.stop // PACK, rows].rearrange(
+                    "p t m j -> p m j t"
+                ),
+                sb(name).rearrange("p j (m t) -> p m j t", t=PACK),
                 ACT.Copy,
             )
 
         def quantise_w1(a):
-            w1_codes.append(sb([P, H], U32, "w1_codes%d" % a))
-            w1_sc.append(sb([P, H], U8, "w1_sc%d" % a))
             nc.vector.quantize_mx(
-                out=w1_codes[a][:].bitcast(FP8X4),
-                scales=w1_sc[a][:],
-                in_=w1_bf[a][:].rearrange("p t m j -> p (t m j)"),
+                out=sb("w1_codes%d" % a).bitcast(FP8X4),
+                scales=sb("w1_sc%d" % a),
+                in_=sb("w1_bf%d" % a).rearrange("p t m j -> p (t m j)"),
             )
 
-        tab = []
+        def load_table(a):
+            nc.sync.dma_start(sb("tab%d" % a).bitcast(I32), tab_words[a].bitcast(I32))
 
-        def load_table(a, tile):
-            tab.append(tile)
-            nc.sync.dma_start(tab[a][:].bitcast(I32), tab_words[a].bitcast(I32))
-
-        load_w1(0, placed([P, PACK // 2, H], F32, "w1_first", 40960)[:], slice(0, PACK // 2), slice(0, H))
-        bias = placed([P, PACK], F32, "bias", 29696)
-        nc.sync.dma_start(bias[:], b1.rearrange("(p t) -> p t", t=PACK))
-        load_table(0, placed([P, T], U16, "tab0", 0))
-        load_w1(0, placed([P, PACK // 2, H], F32, "w1_second", 24576)[:], slice(PACK // 2, PACK), slice(0, H))
-        w1_rest = placed([P, 2, PACK, H // 2], F32, "w1_rest", 8192)
-        for c in range(2):
-            load_w1(1, w1_rest[:, c], slice(0, PACK), slice(c * H // 2, (c + 1) * H // 2))
-        load_table(1, placed([P, T], U16, "tab1", 16384))
-        wd_raw = placed([P, N // 2], I32, "wd_raw", 30720)[:]
-        nc.sync.dma_start(wd_raw, wd_words[0].bitcast(I32))
+        load_w1(0, "w1_first", slice(0, PACK // 2), slice(0, H))
+        nc.sync.dma_start(sb("bias"), b1.rearrange("(p t) -> p t", t=PACK))
+        load_w1(0, "w1_second", slice(PACK // 2, PACK), slice(0, H))
+        load_table(0)
+        load_w1(1, "w1_third", slice(0, PACK), slice(0, H // 2))
+        load_w1(1, "w1_fourth", slice(0, PACK), slice(H // 2, H))
+        load_table(1)
+        nc.sync.dma_start(sb("wd_raw"), wd_words[0].bitcast(I32))
 
         v_sc = []
         for n in range(2):
-            v_sc_lo = sb([P, S], U8, "v_sc_lo%d" % n)
-            nc.vector.tensor_copy(v_sc_lo[:], tab_sc[:].indirect(idx[n][:]))
-            moved = v_sc_hi[:, n * S : (n + 1) * S]
-            nc.sync.dma_start(moved.bitcast(I32)[0 : P - SHIFT, :], v_sc_lo[:].bitcast(I32)[SHIFT:P, :])
-            v_sc.append((v_sc_lo[:], moved))
+            v_sc_lo = sb("v_sc_lo%d" % n)
+            nc.vector.tensor_copy(v_sc_lo, sb("tab_sc").indirect(idx[n][:]))
+            moved = sb("v_sc_hi")[:, n * S : (n + 1) * S]
+            nc.sync.dma_start(moved.bitcast(I32)[0 : P - SHIFT, :], v_sc_lo.bitcast(I32)[SHIFT:P, :])
+            v_sc.append((v_sc_lo, moved))
 
         def deal(out, in_, copy=nc.gpsimd.tensor_copy):
             copy(
@@ -129,210 +194,209 @@ def tile_list_cocitation_drift_backward_kernel(
                 in_.rearrange("p (u m t) -> p u t m", t=PACK, m=P),
             )
 
-        v = {}
-
-        def gather(n, a, half, tag=None, offset=None):
-            name = "v%d%d%d" % (n, a, half)
-            v[n, a, half] = sb([P, HALF], U16, name, tag) if offset is None else placed([P, HALF], U16, name, offset)
+        def gather(n, a, half):
             columns = slice(half * HALF // 16, (half + 1) * HALF // 16)
-            nc.vector.tensor_copy(v[n, a, half][:], tab[a][:].indirect(idx[n][:, columns]))
+            nc.vector.tensor_copy(sb("v%d%d%d" % (n, a, half)), sb("tab%d" % a).indirect(idx[n][:, columns]))
+
+        def bank(number, shape, name):
+            return psum.tile([P] + shape, F32, name=name, tag="bank%d" % number)
 
         pre = {}
 
-        def hidden_matmuls(half, order):
-            entries = slice(half * HALF, (half + 1) * HALF)
+        def hidden(half, order):
             for t in range(PACK):
-                pre[half, t] = psum.tile([P, HALF], F32, name="pre%d%d" % (half, t), tag="bank%d" % t)
+                pre[half, t] = bank(t, [HALF], "pre%d%d" % (half, t))
             for a, t in order:
                 units = slice(t * P, (t + 1) * P)
                 nc.tensor.matmul_mx(
                     out=pre[half, t][:],
-                    lhsT=w1_codes[a][:, units].bitcast(FP8X4),
-                    lhsT_scale=w1_sc[a][:, units],
-                    rhs=v[0, a, half][:].bitcast(FP4X4),
-                    rhs_scale=v_sc[0][a][:, entries],
+                    lhsT=sb("w1_codes%d" % a)[:, units].bitcast(FP8X4),
+                    lhsT_scale=sb("w1_sc%d" % a)[:, units],
+                    rhs=sb("v0%d%d" % (a, half)).bitcast(FP4X4),
+                    rhs_scale=v_sc[0][a][:, half * HALF : (half + 1) * HALF],
                     start=(a == 0),
                     stop=(a == PASSES - 1),
                 )
 
-        gather(0, 0, 0)
-        quantise_w1(0)
-        gather(0, 0, 1, offset=45056)
-        quantise_w1(1)
-        gather(0, 1, 0, offset=57344)
-        gather(0, 1, 1)
-        gather(1, 1, 0)
-
-        wb_sc = sb([P, PASSES * H], U8, "wb_sc")
-        deal(wb_sc[:], w_sc_raw[:, :N])
-        wd_sc = []
-        for g in range(GROUPS):
-            wd_sc.append(placed([P, GROUP], U8, "wd_sc%d" % g, 46080 + 4096 * g))
-            deal(wd_sc[g][:], w_sc_raw[:, N + g * GROUP : N + (g + 1) * GROUP])
-        wb = []
-        for a in range(PASSES):
-            wb_raw = placed([P, H], I32, "wb_raw%d" % a, 24576 + 2048 * a)
-            nc.sync.dma_start(wb_raw[:], wb_words[a].rearrange("p c i -> p (c i)").bitcast(I32))
-            wb.append(sb([P, H], I32, "wb%d" % a))
-            deal(wb[a][:], wb_raw[:])
-        hidden_matmuls(0, [(a, t) for a in range(PASSES) for t in range(PACK)])
-        gather(1, 0, 0, offset=57344 - 960)
-        gather(1, 0, 1, offset=57344 + 960)
-        wd = sb([P, N], U16, "wd")
-        deal(wd[:], wd_raw.bitcast(U16), nc.scalar.copy)
-
-        tanh = {}
-
         def take_tanh(half):
-            if half == 0:
-                tanh[half] = placed([P, PACK, HALF], F32, "tanh0", 32704)
-            else:
-                tanh[half] = sb([P, PACK, HALF], F32, "tanh1")
             for t in range(PACK):
-                nc.scalar.activation(tanh[half][:, t, :], pre[half, t][:], ACT.Tanh, bias=bias[:, t : t + 1])
+                nc.scalar.activation(
+                    sb("tanh%d" % half)[:, t, :], pre[half, t][:], ACT.Tanh, bias=sb("bias")[:, t : t + 1]
+                )
 
-        squares = {}
-
-        def square_on_gpsimd(q, b, tile):
+        def tanh_block(q, b):
             half, part = divmod(q, 2)
             first = part * QUARTER + b * BLOCK
-            rows = tanh[half][:, :, first : first + BLOCK].rearrange("p t j -> p j t")
-            squares[q, b] = tile[:]
-            nc.gpsimd.tensor_tensor(tile[:], rows, rows, ALU.mult)
+            return sb("tanh%d" % half)[:, :, first : first + BLOCK]
 
-        def square(q, blocks, tag=None):
-            half, part = divmod(q, 2)
-            first = part * QUARTER + blocks[0] * BLOCK
-            tile = sb([P, len(blocks) * BLOCK * PACK], F32, "tanh_sq%d%d" % (q, blocks[0]), tag)
+        def square(q, b):
             nc.scalar.activation(
-                tile[:].rearrange("p (c i t) -> p c t i", i=4, t=PACK),
-                tanh[half][:, :, first : first + len(blocks) * BLOCK].rearrange("p t (c i) -> p c t i", i=4),
+                sb("sq%d%d" % (q, b)).rearrange("p (c i) t -> p c t i", i=4),
+                tanh_block(q, b).rearrange("p t (c i) -> p c t i", i=4),
                 ACT.Square,
             )
-            for n, b in enumerate(blocks):
-                words = tile[:, n * BLOCK * PACK : (n + 1) * BLOCK * PACK]
-                squares[q, b] = words.rearrange("p (j t) -> p j t", t=PACK)
 
-        h_codes, h_sc = {}, {}
+        def square_on_gpsimd(q, b):
+            rows = tanh_block(q, b).rearrange("p t j -> p j t")
+            nc.gpsimd.tensor_tensor(sb("sq%d%d" % (q, b)), rows, rows, ALU.mult)
 
-        def make_h(q, banks, neg_h=None, passes=(0, 1)):
-            if neg_h is None:
-                neg_h = sb([P, QUARTER * PACK], BF16, "neg_h%d" % q)
-            for b in range(QUARTER // BLOCK):
-                first = q * QUARTER + b * BLOCK
-                half, inside = divmod(first, HALF)
-                err = psum.tile([P, PACK, BLOCK], F32, name="err%d%d" % (q, b), tag="bank%d" % banks[b])
+        err = {}
+
+        def errors(q, banks, passes=(0, 1)):
+            half, part = divmod(q, 2)
+            for b in range(2):
+                inside = part * QUARTER + b * BLOCK
+                first = half * HALF + inside
+                err[q, b] = bank(banks[b], [PACK, BLOCK], "err%d%d" % (q, b))
                 for a in passes:
                     for t in range(PACK):
-                        units = slice(a * H + t * P, a * H + (t + 1) * P)
                         nc.tensor.matmul_mx(
-                            out=err[:, t, :],
-                            lhsT=wb[a][:, t * P : (t + 1) * P].bitcast(FP8X4),
-                            lhsT_scale=wb_sc[:, units],
-                            rhs=v[1, a, half][:, inside : inside + BLOCK].bitcast(FP4X4),
+                            out=err[q, b][:, t, :],
+                            lhsT=sb("wb%d" % a)[:, t * P : (t + 1) * P].bitcast(FP8X4),
+                            lhsT_scale=sb("wb_sc")[:, a * H + t * P : a * H + (t + 1) * P],
+                            rhs=sb("v1%d%d" % (a, half))[:, inside : inside + BLOCK].bitcast(FP4X4),
                             rhs_scale=v_sc[1][a][:, first : first + BLOCK],
                             start=(a == passes[0] and t == 0),
                             stop=(a == passes[-1] and t == PACK - 1),
                         )
-                words = slice(b * BLOCK * PACK, (b + 1) * BLOCK * PACK)
+
+        def make_h(q):
+            neg_h = sb("neg_h%d" % q)
+            for b in range(2):
                 nc.vector.scalar_tensor_tensor(
-                    out=neg_h[:, words].rearrange("p (j t) -> p j t", t=PACK),
-                    in0=squares[q, b],
+                    out=neg_h[:, b * BLOCK * PACK : (b + 1) * BLOCK * PACK].rearrange("p (j t) -> p j t", t=PACK),
+                    in0=sb("sq%d%d" % (q, b)),
                     scalar=1.0,
-                    in1=err[:].rearrange("p t j -> p j t"),
+                    in1=err[q, b][:].rearrange("p t j -> p j t"),
                     op0=ALU.subtract,
                     op1=ALU.mult,
                 )
-            h_codes[q] = sb([P, QUARTER], U32, "h_codes%d" % q)
-            h_sc[q] = sb([P, QUARTER], U8, "h_sc%d" % q)
-            for b in range(QUARTER // BLOCK):
+            for b in range(2):
                 nc.vector.quantize_mx(
-                    out=h_codes[q][:, b * BLOCK : (b + 1) * BLOCK].bitcast(FP8X4),
-                    scales=h_sc[q][:, b * BLOCK : (b + 1) * BLOCK],
+                    out=sb("h_codes%d" % q)[:, b * BLOCK : (b + 1) * BLOCK].bitcast(FP8X4),
+                    scales=sb("h_sc%d" % q)[:, b * BLOCK : (b + 1) * BLOCK],
                     in_=neg_h[:, b * BLOCK * PACK : (b + 1) * BLOCK * PACK],
                 )
 
         y_rows = out_0.rearrange("(g p t) j -> g p t j", p=P, t=PACK)
         y_words = out_1.rearrange("g p m t -> p g (m t)").bitcast(I32)
-        y_sc = sb([P, GROUPS * S], U8, "y_sc")
-        y = {}
+        acc = {}
 
-        def make_y(q, groups, banks):
-            entries = slice(q * QUARTER, (q + 1) * QUARTER)
-            for g in groups:
-                y[q, g] = sb([P, PACK, QUARTER], F32, "y%d%d" % (q, g))
-                for pair in range(PACK // 2):
-                    acc = psum.tile([P, 2, QUARTER], F32, name="acc%d%d%d" % (q, g, pair), tag="bank%d" % banks[pair])
-                    for u in range(2):
-                        first = g * GROUP + (2 * pair + u) * P
-                        nc.tensor.matmul_mx(
-                            out=acc[:, u, :],
-                            lhsT=wd[:, first : first + P].bitcast(FP4X4),
-                            lhsT_scale=wd_sc[g][:, first - g * GROUP : first - g * GROUP + P],
-                            rhs=h_codes[q][:].bitcast(FP8X4),
-                            rhs_scale=h_sc[q][:],
-                            start=True,
-                            stop=True,
-                        )
-                    for u in range(2):
-                        t = 2 * pair + u
-                        factor = neg_gain[:, g * PACK + t : g * PACK + t + 1]
-                        nc.scalar.activation(y[q, g][:, t, :], acc[:, u, :], ACT.Copy, scale=factor)
-                nc.sync.dma_start(y_rows[g][:, :, entries], y[q, g][:])
-
-        def make_planes(q, y_bf=None, shared=()):
-            entries = slice(q * QUARTER, (q + 1) * QUARTER)
-            y_codes = sb([P, GROUPS * QUARTER], U32, "y_codes%d" % q)
-            y_bf = y_bf or [sb([P, QUARTER * PACK], BF16, "y_bf%d%d" % (q, g)) for g in range(GROUPS)]
-            for g in range(GROUPS):
-                copies = (nc.vector.tensor_copy, nc.scalar.copy) if g in shared else (nc.vector.tensor_copy,)
-                width = QUARTER // len(copies)
-                for n, copy in enumerate(copies):
-                    words = y_bf[g][:, n * width * PACK : (n + 1) * width * PACK]
-                    copy(
-                        words.rearrange("p (c i t) -> p c t i", i=4, t=PACK),
-                        y[q, g][:, :, n * width : (n + 1) * width].rearrange("p t (c i) -> p c t i", i=4),
+        def multiply_y(q, g, banks):
+            for pair in range(PACK // 2):
+                acc[q, g, pair] = bank(banks[pair], [2, QUARTER], "acc%d%d%d" % (q, g, pair))
+                for u in range(2):
+                    first = (2 * pair + u) * P
+                    nc.tensor.matmul_mx(
+                        out=acc[q, g, pair][:, u, :],
+                        lhsT=sb("wd")[:, g * GROUP + first : g * GROUP + first + P].bitcast(FP4X4),
+                        lhsT_scale=sb("wd_sc%d" % g)[:, first : first + P],
+                        rhs=sb("h_codes%d" % q).bitcast(FP8X4),
+                        rhs_scale=sb("h_sc%d" % q),
+                        start=True,
+                        stop=True,
                     )
-            for g in range(GROUPS):
-                nc.vector.quantize_mx(
-                    out=y_codes[:, g * QUARTER : (g + 1) * QUARTER].bitcast(FP8X4),
-                    scales=y_sc[:, g * S + q * QUARTER : g * S + (q + 1) * QUARTER],
-                    in_=y_bf[g][:],
+
+        def empty_y(q, g):
+            y = sb("y%d%d" % (q, g))
+            for t in range(PACK):
+                factor = sb("neg_gain")[:, g * PACK + t : g * PACK + t + 1]
+                nc.scalar.activation(y[:, t, :], acc[q, g, t // 2][:, t % 2, :], ACT.Copy, scale=factor)
+            nc.sync.dma_start(y_rows[g][:, :, q * QUARTER : (q + 1) * QUARTER], y)
+
+        def weave(q, g, copies=(nc.vector.tensor_copy,)):
+            width = QUARTER // len(copies)
+            for n, copy in enumerate(copies):
+                copy(
+                    sb("y_bf%d%d" % (q, g))[:, n * width * PACK : (n + 1) * width * PACK].rearrange(
+                        "p (c i t) -> p c t i", i=4, t=PACK
+                    ),
+                    sb("y%d%d" % (q, g))[:, :, n * width : (n + 1) * width].rearrange("p t (c i) -> p c t i", i=4),
                 )
-            nc.sync.dma_start(
-                y_words[:, :, entries], y_codes[:].bitcast(I32).rearrange("p (g m) -> p g m", g=GROUPS)
+
+        def quantise_y(q, g):
+            nc.vector.quantize_mx(
+                out=sb("y_codes%d" % q)[:, g * QUARTER : (g + 1) * QUARTER].bitcast(FP8X4),
+                scales=sb("y_sc")[:, g * S + q * QUARTER : g * S + (q + 1) * QUARTER],
+                in_=sb("y_bf%d%d" % (q, g)),
             )
 
+        def store_codes(q):
+            nc.sync.dma_start(
+                y_words[:, :, q * QUARTER : (q + 1) * QUARTER],
+                sb("y_codes%d" % q).bitcast(I32).rearrange("p (g m) -> p g m", g=GROUPS),
+            )
+
+        def make_y(q, g, banks):
+            multiply_y(q, g, banks)
+            empty_y(q, g)
+
+        def make_planes(q, last=(nc.vector.tensor_copy,)):
+            weave(q, 0)
+            weave(q, 1, last)
+            quantise_y(q, 0)
+            quantise_y(q, 1)
+            store_codes(q)
+
+        quantise_w1(0)
+        gather(0, 0, 0)
+        gather(0, 0, 1)
+        quantise_w1(1)
+        gather(0, 1, 0)
+        gather(0, 1, 1)
+        gather(1, 1, 0)
+
+        deal(sb("wb_sc"), sb("w_sc_raw")[:, :N])
+        for g in range(GROUPS):
+            deal(sb("wd_sc%d" % g), sb("w_sc_raw")[:, N + g * GROUP : N + (g + 1) * GROUP])
+        for a in range(PASSES):
+            nc.sync.dma_start(sb("wb_raw%d" % a), wb_words[a].rearrange("p c i -> p (c i)").bitcast(I32))
+            deal(sb("wb%d" % a), sb("wb_raw%d" % a))
+        hidden(0, [(a, t) for a in range(PASSES) for t in range(PACK)])
+        gather(1, 0, 0)
+        gather(1, 0, 1)
+        deal(sb("wd"), sb("wd_raw").bitcast(U16), nc.scalar.copy)
+
         take_tanh(0)
-        square(0, (0, 1))
-        square_on_gpsimd(1, 0, placed([P, BLOCK, PACK], F32, "tanh_sq10", 26624))
-        hidden_matmuls(1, [(a, t) for t in range(PACK) for a in range(PASSES)])
+        square(0, 0)
+        square(0, 1)
+        square_on_gpsimd(1, 0)
+        hidden(1, [(a, t) for t in range(PACK) for a in range(PASSES)])
         take_tanh(1)
-        square(2, (0,))
-        make_h(0, (4, 5), placed([P, QUARTER * PACK], BF16, "neg_h0", 53248), passes=(1, 0))
-        square_on_gpsimd(1, 1, placed([P, BLOCK, PACK], F32, "tanh_sq11", 54272))
-        make_y(0, (0,), (4, 5))
-        make_y(0, (1,), (0, 1))
-        gather(1, 1, 1, offset=53248)
-        make_h(1, (6, 7), passes=(1, 0))
-        square(2, (1,), "h_codes0")
-        make_y(1, (0,), (2, 3))
-        make_planes(0, [placed([P, QUARTER * PACK], BF16, "y_bf00", 54272), sb([P, QUARTER * PACK], BF16, "y_bf01", "neg_h1")])
-        make_h(2, (6, 7))
-        square(3, (0, 1), "h_sc1")
-        make_y(1, (1,), (4, 5))
-        make_h(3, (6, 7))
-        make_y(2, (0,), (0, 1))
-        make_y(2, (1,), (2, 3))
-        make_planes(1)
-        make_y(3, (0,), (4, 5))
-        make_y(3, (1,), (0, 1))
+        square(2, 0)
+        errors(0, (4, 5), (1, 0))
+        make_h(0)
+        square_on_gpsimd(1, 1)
+        make_y(0, 0, (4, 5))
+        make_y(0, 1, (0, 1))
+        gather(1, 1, 1)
+        errors(1, (6, 7), (1, 0))
+        make_h(1)
+        square(2, 1)
+        make_y(1, 0, (2, 3))
+        make_planes(0)
+        errors(2, (6, 7))
+        make_h(2)
+        make_y(1, 1, (4, 5))
+        square(3, 0)
+        square(3, 1)
+        weave(1, 0)
+        weave(1, 1)
+        errors(3, (6, 7))
+        make_y(2, 0, (0, 1))
+        make_y(2, 1, (2, 3))
+        make_h(3)
+        quantise_y(1, 0)
+        quantise_y(1, 1)
+        store_codes(1)
+        make_y(3, 0, (4, 5))
+        make_y(3, 1, (0, 1))
         make_planes(2)
-        make_planes(3, shared=(1,))
+        make_planes(3, (nc.vector.tensor_copy, nc.scalar.copy))
 
         sc_rows = out_2.bitcast(I32).rearrange("g (q r) c -> r q g c", r=4)
         for r in range(4):
             queue = nc.sync if r % 2 == 0 else nc.scalar
             queue.dma_start(
-                sc_rows[r], y_sc[:].bitcast(I32)[r:P:32, :].rearrange("q (g c) -> q g c", g=GROUPS)
+                sc_rows[r], sb("y_sc").bitcast(I32)[r:P:32, :].rearrange("q (g c) -> q g c", g=GROUPS)
             )

@@ -29,7 +29,8 @@ ALIGN = 64
 
 TILES = {
     "tab_sc": (U8, 1, [T]),
-    "w_sc_raw": (U8, 1, [2 * N]),
+    "wb_sc_raw": (U8, 1, [PASSES * H]),
+    "wd_sc_raw": (U8, 1, [N]),
     "v_sc_hi": (U8, 1, [2 * S]),
     "gain_raw": (F32, 4, [GROUPS, PACK]),
     "neg_gain": (F32, 4, [GROUPS * PACK]),
@@ -64,10 +65,9 @@ TILES = {
 HEIRS = {
     "gain_raw": ["bias", "w1_second", "tab0", "w1_third", "w1_fourth", "tab1", "wd_raw"],
     "w1_second": ["v001", "wb_raw0", "wb_raw1"],
-    "wb_raw1": ["sq10"],
+    "wb_raw1": ["wd_sc1", "sq10"],
     "wd_raw": ["tanh0"],
     "w1_bf0": ["wd_sc0"],
-    "w1_bf1": ["wd_sc1"],
     "v010": ["v100", "v101"],
     "sq01": ["v111"],
     "neg_h0": ["sq11"],
@@ -126,7 +126,7 @@ def tile_list_cocitation_drift_backward_kernel(
 
         idx = [lists.tile([P, S // 16], U16, name="idx%d" % n) for n in range(2)]
 
-        for name in ("tab_sc", "w_sc_raw", "v_sc_hi"):
+        for name in ("tab_sc", "wb_sc_raw", "wd_sc_raw", "v_sc_hi"):
             nc.vector.memset(sb(name).bitcast(I32), 0)
 
         nc.sync.dma_start(sb("gain_raw"), gain.rearrange("(g p t) -> p g t", p=P, t=PACK))
@@ -140,10 +140,10 @@ def tile_list_cocitation_drift_backward_kernel(
         wd_rows = wd_scales[0].bitcast(I32).rearrange("(q r) c -> r q c", r=4)
         for r in range(4):
             nc.gpsimd.dma_start(
-                sb("w_sc_raw")[:, :N].bitcast(I32)[r:P:32, :].rearrange("q (a c) -> q a c", a=PASSES), wb_rows[r]
+                sb("wb_sc_raw").bitcast(I32)[r:P:32, :].rearrange("q (a c) -> q a c", a=PASSES), wb_rows[r]
             )
         for r in range(4):
-            nc.gpsimd.dma_start(sb("w_sc_raw")[:, N:].bitcast(I32)[r:P:32, :], wd_rows[r])
+            nc.gpsimd.dma_start(sb("wd_sc_raw").bitcast(I32)[r:P:32, :], wd_rows[r])
 
         nc.scalar.activation(
             sb("neg_gain").rearrange("p (g t) -> p g t", t=PACK), sb("gain_raw"), ACT.Copy, scale=-1.0
@@ -172,12 +172,12 @@ def tile_list_cocitation_drift_backward_kernel(
             nc.sync.dma_start(sb("tab%d" % a).bitcast(I32), tab_words[a].bitcast(I32))
 
         load_w1(0, "w1_first", slice(0, PACK // 2), slice(0, H))
-        nc.sync.dma_start(sb("bias"), b1.rearrange("(p t) -> p t", t=PACK))
         load_w1(0, "w1_second", slice(PACK // 2, PACK), slice(0, H))
         load_table(0)
         load_w1(1, "w1_third", slice(0, PACK), slice(0, H // 2))
         load_w1(1, "w1_fourth", slice(0, PACK), slice(H // 2, H))
         load_table(1)
+        nc.sync.dma_start(sb("bias"), b1.rearrange("(p t) -> p t", t=PACK))
         nc.sync.dma_start(sb("wd_raw"), wd_words[0].bitcast(I32))
 
         v_sc = []
@@ -218,8 +218,8 @@ def tile_list_cocitation_drift_backward_kernel(
                     stop=(a == PASSES - 1),
                 )
 
-        def take_tanh(half):
-            for t in range(PACK):
+        def take_tanh(half, slices=range(PACK)):
+            for t in slices:
                 nc.scalar.activation(
                     sb("tanh%d" % half)[:, t, :], pre[half, t][:], ACT.Tanh, bias=sb("bias")[:, t : t + 1]
                 )
@@ -346,23 +346,27 @@ def tile_list_cocitation_drift_backward_kernel(
         gather(0, 1, 1)
         gather(1, 1, 0)
 
-        deal(sb("wb_sc"), sb("w_sc_raw")[:, :N])
-        for g in range(GROUPS):
-            deal(sb("wd_sc%d" % g), sb("w_sc_raw")[:, N + g * GROUP : N + (g + 1) * GROUP])
+        def deal_wd_scales(g):
+            deal(sb("wd_sc%d" % g), sb("wd_sc_raw")[:, g * GROUP : (g + 1) * GROUP])
+
+        deal(sb("wb_sc"), sb("wb_sc_raw"))
+        deal_wd_scales(0)
         for a in range(PASSES):
             nc.sync.dma_start(sb("wb_raw%d" % a), wb_words[a].rearrange("p c i -> p (c i)").bitcast(I32))
             deal(sb("wb%d" % a), sb("wb_raw%d" % a))
+        deal_wd_scales(1)
         hidden(0, [(a, t) for a in range(PASSES) for t in range(PACK)])
         gather(1, 0, 0)
         gather(1, 0, 1)
         deal(sb("wd"), sb("wd_raw").bitcast(U16), nc.scalar.copy)
 
         take_tanh(0)
+        hidden(1, [(a, t) for t in range(PACK) for a in range(PASSES)])
+        take_tanh(1, range(1))
         square(0, 0)
         square(0, 1)
         square_on_gpsimd(1, 0)
-        hidden(1, [(a, t) for t in range(PACK) for a in range(PASSES)])
-        take_tanh(1)
+        take_tanh(1, range(1, PACK))
         square(2, 0)
         errors(0, (4, 5), (1, 0))
         make_h(0)

@@ -302,7 +302,9 @@ def tile_list_cocitation_drift_backward_kernel(
             for t in range(PACK):
                 factor = sb("neg_gain")[:, g * PACK + t : g * PACK + t + 1]
                 nc.scalar.activation(y[:, t, :], acc[q, g, t // 2][:, t % 2, :], ACT.Copy, scale=factor)
-            nc.sync.dma_start(y_rows[g][:, :, q * QUARTER : (q + 1) * QUARTER], y)
+                if t % 2 == 1:
+                    rows = slice(t - 1, t + 1)
+                    nc.sync.dma_start(y_rows[g][:, rows, q * QUARTER : (q + 1) * QUARTER], y[:, rows, :])
 
         def weave(q, g, copies=(nc.vector.tensor_copy,)):
             width = QUARTER // len(copies)
@@ -321,19 +323,19 @@ def tile_list_cocitation_drift_backward_kernel(
                 in_=sb("y_bf%d%d" % (q, g)),
             )
 
-        def store_codes(q):
+        def store_codes(q, groups=slice(0, GROUPS)):
             nc.sync.dma_start(
-                y_words[:, :, q * QUARTER : (q + 1) * QUARTER],
-                sb("y_codes%d" % q).bitcast(I32).rearrange("p (g m) -> p g m", g=GROUPS),
+                y_words[:, groups, q * QUARTER : (q + 1) * QUARTER],
+                sb("y_codes%d" % q).bitcast(I32).rearrange("p (g m) -> p g m", g=GROUPS)[:, groups, :],
             )
 
         def make_y(q, g, banks):
             multiply_y(q, g, banks)
             empty_y(q, g)
 
-        def make_planes(q, last=(nc.vector.tensor_copy,)):
+        def make_planes(q):
             weave(q, 0)
-            weave(q, 1, last)
+            weave(q, 1)
             quantise_y(q, 0)
             quantise_y(q, 1)
             store_codes(q)
@@ -396,7 +398,11 @@ def tile_list_cocitation_drift_backward_kernel(
         make_y(3, 0, (4, 5))
         make_y(3, 1, (0, 1))
         make_planes(2)
-        make_planes(3, (nc.vector.tensor_copy, nc.scalar.copy))
+        weave(3, 0)
+        weave(3, 1, (nc.vector.tensor_copy, nc.scalar.copy))
+        for g in range(GROUPS):
+            quantise_y(3, g)
+            store_codes(3, slice(g, g + 1))
 
         sc_rows = out_2.bitcast(I32).rearrange("g (q r) c -> r q g c", r=4)
         for r in range(4):

@@ -37,8 +37,8 @@ TILES = {
     "bias": (F32, 4, [PACK]),
     "w1_first": (F32, 4, [PACK // 2, H]),
     "w1_second": (F32, 4, [PACK // 2, H]),
-    "w1_third": (F32, 4, [PACK, H // 2]),
-    "w1_fourth": (F32, 4, [PACK, H // 2]),
+    "w1_third": (F32, 4, [PACK // 2, H]),
+    "w1_fourth": (F32, 4, [PACK // 2, H]),
     "wd_raw": (I32, 4, [N // 2]),
     "wd": (U16, 2, [N]),
     "wb_sc": (U8, 1, [PASSES * H]),
@@ -63,18 +63,22 @@ TILES = {
 }
 
 HEIRS = {
-    "gain_raw": ["bias", "w1_second", "tab0", "w1_third", "w1_fourth", "tab1", "wd_raw"],
+    "gain_raw": ["bias", "w1_second", "w1_third", "tab0", "w1_fourth", "tab1", "wd_raw"],
     "w1_second": ["v001", "wb_raw0", "wb_raw1"],
     "wb_raw1": ["wd_sc1", "sq10"],
     "wd_raw": ["tanh0"],
+    "w1_fourth": ["v010", "v011", "v110"],
     "w1_bf0": ["wd_sc0"],
     "v010": ["v100", "v101"],
     "sq01": ["v111"],
     "neg_h0": ["sq11"],
-    "sq11": ["y_bf00"],
-    "neg_h1": ["y_bf01"],
+    "sq11": ["sq20", "y_bf00"],
     "h_codes0": ["sq21"],
+    "sq21": ["y_bf01", "y_codes0"],
     "h_sc1": ["sq30", "sq31"],
+    "y_bf00": ["neg_h3"],
+    "sq31": ["y_bf10", "y_bf11", "y_bf20"],
+    "h_sc3": ["y_bf30"],
 }
 
 
@@ -151,31 +155,33 @@ def tile_list_cocitation_drift_backward_kernel(
 
         w1_rows = w1.rearrange("(a p j) c -> a p j c", p=P, j=PACK)
 
-        def load_w1(a, name, rows, columns):
-            nc.sync.dma_start(sb(name), w1_rows[a][:, rows, columns])
-            nc.scalar.activation(
-                sb("w1_bf%d" % a)[:, :, columns.start // PACK : columns.stop // PACK, rows].rearrange(
-                    "p t m j -> p m j t"
-                ),
-                sb(name).rearrange("p j (m t) -> p m j t", t=PACK),
-                ACT.Copy,
+        def load_w1(a, name, rows, parts=(slice(0, PACK),)):
+            nc.sync.dma_start(sb(name), w1_rows[a][:, rows, :])
+            for slices in parts:
+                nc.scalar.activation(
+                    sb("w1_bf%d" % a)[:, slices, :, rows].rearrange("p t m j -> p m j t"),
+                    sb(name).rearrange("p j (m t) -> p m j t", t=PACK)[:, :, :, slices],
+                    ACT.Copy,
+                )
+
+        def quantise_w1(a, slices=slice(0, PACK)):
+            units = slice(slices.start * P, slices.stop * P)
+            nc.vector.quantize_mx(
+                out=sb("w1_codes%d" % a)[:, units].bitcast(FP8X4),
+                scales=sb("w1_sc%d" % a)[:, units],
+                in_=sb("w1_bf%d" % a)[:, slices].rearrange("p t m j -> p (t m j)"),
             )
 
-        def quantise_w1(a):
-            nc.vector.quantize_mx(
-                out=sb("w1_codes%d" % a).bitcast(FP8X4),
-                scales=sb("w1_sc%d" % a),
-                in_=sb("w1_bf%d" % a).rearrange("p t m j -> p (t m j)"),
-            )
+        pairs = (slice(0, PACK // 2), slice(PACK // 2, PACK))
 
         def load_table(a):
             nc.sync.dma_start(sb("tab%d" % a).bitcast(I32), tab_words[a].bitcast(I32))
 
-        load_w1(0, "w1_first", slice(0, PACK // 2), slice(0, H))
-        load_w1(0, "w1_second", slice(PACK // 2, PACK), slice(0, H))
+        load_w1(0, "w1_first", pairs[0])
+        load_w1(0, "w1_second", pairs[1])
+        load_w1(1, "w1_third", pairs[0])
         load_table(0)
-        load_w1(1, "w1_third", slice(0, PACK), slice(0, H // 2))
-        load_w1(1, "w1_fourth", slice(0, PACK), slice(H // 2, H))
+        load_w1(1, "w1_fourth", pairs[1], pairs)
         load_table(1)
         nc.sync.dma_start(sb("bias"), b1.rearrange("(p t) -> p t", t=PACK))
         nc.sync.dma_start(sb("wd_raw"), wd_words[0].bitcast(I32))
@@ -235,6 +241,10 @@ def tile_list_cocitation_drift_backward_kernel(
                 tanh_block(q, b).rearrange("p t (c i) -> p c t i", i=4),
                 ACT.Square,
             )
+
+        def square_on_vector(q, b):
+            rows = tanh_block(q, b).rearrange("p t (c i) -> p c t i", i=4)
+            nc.vector.tensor_tensor(sb("sq%d%d" % (q, b)).rearrange("p (c i) t -> p c t i", i=4), rows, rows, ALU.mult)
 
         def square_on_gpsimd(q, b):
             rows = tanh_block(q, b).rearrange("p t j -> p j t")
@@ -343,7 +353,8 @@ def tile_list_cocitation_drift_backward_kernel(
         quantise_w1(0)
         gather(0, 0, 0)
         gather(0, 0, 1)
-        quantise_w1(1)
+        for slices in pairs:
+            quantise_w1(1, slices)
         gather(0, 1, 0)
         gather(0, 1, 1)
         gather(1, 1, 0)
@@ -369,7 +380,6 @@ def tile_list_cocitation_drift_backward_kernel(
         square(0, 1)
         square_on_gpsimd(1, 0)
         take_tanh(1, range(1, PACK))
-        square(2, 0)
         errors(0, (4, 5), (1, 0))
         make_h(0)
         square_on_gpsimd(1, 1)
@@ -379,28 +389,29 @@ def tile_list_cocitation_drift_backward_kernel(
         errors(1, (6, 7), (1, 0))
         make_h(1)
         square(2, 1)
+        square_on_vector(2, 0)
+        weave(0, 0)
         make_y(1, 0, (2, 3))
-        make_planes(0)
-        errors(2, (6, 7))
-        make_h(2)
         make_y(1, 1, (4, 5))
+        errors(2, (6, 7))
         square(3, 0)
         square(3, 1)
-        weave(1, 0)
-        weave(1, 1)
+        make_h(2)
+        weave(0, 1)
+        quantise_y(0, 0)
+        quantise_y(0, 1)
+        store_codes(0)
         errors(3, (6, 7))
         make_y(2, 0, (0, 1))
-        make_y(2, 1, (2, 3))
         make_h(3)
-        quantise_y(1, 0)
-        quantise_y(1, 1)
-        store_codes(1)
+        make_y(2, 1, (6, 7))
         make_y(3, 0, (4, 5))
-        make_y(3, 1, (0, 1))
+        make_y(3, 1, (2, 3))
+        make_planes(1)
         make_planes(2)
-        weave(3, 0)
-        weave(3, 1, (nc.vector.tensor_copy, nc.scalar.copy))
-        for g in range(GROUPS):
+        weave(3, 0, (nc.scalar.copy,))
+        weave(3, 1)
+        for g in (1, 0):
             quantise_y(3, g)
             store_codes(3, slice(g, g + 1))
 

@@ -37,8 +37,8 @@ TILES = {
     "bias": (F32, 4, [PACK]),
     "w1_first": (F32, 4, [PACK // 2, H]),
     "w1_second": (F32, 4, [PACK // 2, H]),
-    "w1_third": (F32, 4, [PACK // 2, H]),
-    "w1_fourth": (F32, 4, [PACK // 2, H]),
+    "w1_third": (F32, 4, [PACK, H // 2]),
+    "w1_fourth": (F32, 4, [PACK, H // 2]),
     "wd_raw": (I32, 4, [N // 2]),
     "wd": (U16, 2, [N]),
     "wb_sc": (U8, 1, [PASSES * H]),
@@ -63,11 +63,10 @@ TILES = {
 }
 
 HEIRS = {
-    "gain_raw": ["bias", "w1_second", "w1_third", "tab0", "w1_fourth", "tab1", "wd_raw"],
+    "gain_raw": ["bias", "w1_second", "tab0", "w1_third", "w1_fourth", "tab1", "wd_raw"],
     "w1_second": ["v001", "wb_raw0", "wb_raw1"],
     "wb_raw1": ["wd_sc1", "sq10"],
     "wd_raw": ["tanh0"],
-    "w1_fourth": ["v010", "v011", "v110"],
     "w1_bf0": ["wd_sc0"],
     "v010": ["v100", "v101"],
     "sq01": ["v111"],
@@ -155,33 +154,31 @@ def tile_list_cocitation_drift_backward_kernel(
 
         w1_rows = w1.rearrange("(a p j) c -> a p j c", p=P, j=PACK)
 
-        def load_w1(a, name, rows, parts=(slice(0, PACK),)):
-            nc.sync.dma_start(sb(name), w1_rows[a][:, rows, :])
-            for slices in parts:
-                nc.scalar.activation(
-                    sb("w1_bf%d" % a)[:, slices, :, rows].rearrange("p t m j -> p m j t"),
-                    sb(name).rearrange("p j (m t) -> p m j t", t=PACK)[:, :, :, slices],
-                    ACT.Copy,
-                )
-
-        def quantise_w1(a, slices=slice(0, PACK)):
-            units = slice(slices.start * P, slices.stop * P)
-            nc.vector.quantize_mx(
-                out=sb("w1_codes%d" % a)[:, units].bitcast(FP8X4),
-                scales=sb("w1_sc%d" % a)[:, units],
-                in_=sb("w1_bf%d" % a)[:, slices].rearrange("p t m j -> p (t m j)"),
+        def load_w1(a, name, rows, columns):
+            nc.sync.dma_start(sb(name), w1_rows[a][:, rows, columns])
+            nc.scalar.activation(
+                sb("w1_bf%d" % a)[:, :, columns.start // PACK : columns.stop // PACK, rows].rearrange(
+                    "p t m j -> p m j t"
+                ),
+                sb(name).rearrange("p j (m t) -> p m j t", t=PACK),
+                ACT.Copy,
             )
 
-        pairs = (slice(0, PACK // 2), slice(PACK // 2, PACK))
+        def quantise_w1(a):
+            nc.vector.quantize_mx(
+                out=sb("w1_codes%d" % a).bitcast(FP8X4),
+                scales=sb("w1_sc%d" % a),
+                in_=sb("w1_bf%d" % a).rearrange("p t m j -> p (t m j)"),
+            )
 
         def load_table(a):
             nc.sync.dma_start(sb("tab%d" % a).bitcast(I32), tab_words[a].bitcast(I32))
 
-        load_w1(0, "w1_first", pairs[0])
-        load_w1(0, "w1_second", pairs[1])
-        load_w1(1, "w1_third", pairs[0])
+        load_w1(0, "w1_first", slice(0, PACK // 2), slice(0, H))
+        load_w1(0, "w1_second", slice(PACK // 2, PACK), slice(0, H))
         load_table(0)
-        load_w1(1, "w1_fourth", pairs[1], pairs)
+        load_w1(1, "w1_third", slice(0, PACK), slice(0, H // 2))
+        load_w1(1, "w1_fourth", slice(0, PACK), slice(H // 2, H))
         load_table(1)
         nc.sync.dma_start(sb("bias"), b1.rearrange("(p t) -> p t", t=PACK))
         nc.sync.dma_start(sb("wd_raw"), wd_words[0].bitcast(I32))
@@ -209,9 +206,9 @@ def tile_list_cocitation_drift_backward_kernel(
 
         pre = {}
 
-        def hidden(half, order):
+        def hidden(half, order, banks):
             for t in range(PACK):
-                pre[half, t] = bank(t, [HALF], "pre%d%d" % (half, t))
+                pre[half, t] = bank(banks[t], [HALF], "pre%d%d" % (half, t))
             for a, t in order:
                 units = slice(t * P, (t + 1) * P)
                 nc.tensor.matmul_mx(
@@ -353,8 +350,7 @@ def tile_list_cocitation_drift_backward_kernel(
         quantise_w1(0)
         gather(0, 0, 0)
         gather(0, 0, 1)
-        for slices in pairs:
-            quantise_w1(1, slices)
+        quantise_w1(1)
         gather(0, 1, 0)
         gather(0, 1, 1)
         gather(1, 1, 0)
@@ -368,22 +364,22 @@ def tile_list_cocitation_drift_backward_kernel(
             nc.sync.dma_start(sb("wb_raw%d" % a), wb_words[a].rearrange("p c i -> p (c i)").bitcast(I32))
             deal(sb("wb%d" % a), sb("wb_raw%d" % a))
         deal_wd_scales(1)
-        hidden(0, [(a, t) for a in range(PASSES) for t in range(PACK)])
+        hidden(0, [(a, t) for a in range(PASSES) for t in range(PACK)], (0, 1, 2, 3))
         gather(1, 0, 0)
         gather(1, 0, 1)
         deal(sb("wd"), sb("wd_raw").bitcast(U16), nc.scalar.copy)
 
         take_tanh(0)
-        hidden(1, [(a, t) for t in range(PACK) for a in range(PASSES)])
+        hidden(1, [(a, t) for t in range(PACK) for a in range(PASSES)], (0, 1, 4, 5))
         take_tanh(1, range(1))
         square(0, 0)
         square(0, 1)
         square_on_gpsimd(1, 0)
         take_tanh(1, range(1, PACK))
-        errors(0, (4, 5), (1, 0))
+        errors(0, (2, 3), (1, 0))
         make_h(0)
         square_on_gpsimd(1, 1)
-        make_y(0, 0, (4, 5))
+        make_y(0, 0, (2, 3))
         make_y(0, 1, (0, 1))
         gather(1, 1, 1)
         errors(1, (6, 7), (1, 0))
@@ -391,8 +387,8 @@ def tile_list_cocitation_drift_backward_kernel(
         square(2, 1)
         square_on_vector(2, 0)
         weave(0, 0)
-        make_y(1, 0, (2, 3))
-        make_y(1, 1, (4, 5))
+        make_y(1, 0, (4, 5))
+        make_y(1, 1, (2, 3))
         errors(2, (6, 7))
         square(3, 0)
         square(3, 1)

@@ -67,7 +67,8 @@ HEIRS = {
     "w1_second": ["v001", "wb_raw0", "wb_raw1"],
     "wb_raw1": ["wd_sc1", "sq10"],
     "wd_raw": ["tanh0"],
-    "w1_bf0": ["wd_sc0"],
+    "w1_bf0": ["wb_sc"],
+    "w1_bf1": ["wd_sc0"],
     "v010": ["v100", "v101"],
     "sq01": ["v111"],
     "neg_h0": ["sq11"],

@@ -331,10 +331,10 @@ def tile_list_cocitation_drift_backward_kernel(
                 in_=sb("y_bf%d%d" % (q, g)),
             )
 
-        def store_codes(q, groups=slice(0, GROUPS)):
+        def store_codes(q):
             nc.sync.dma_start(
-                y_words[:, groups, q * QUARTER : (q + 1) * QUARTER],
-                sb("y_codes%d" % q).bitcast(I32).rearrange("p (g m) -> p g m", g=GROUPS)[:, groups, :],
+                y_words[:, :, q * QUARTER : (q + 1) * QUARTER],
+                sb("y_codes%d" % q).bitcast(I32).rearrange("p (g m) -> p g m", g=GROUPS),
             )
 
         def make_y(q, g, banks):
@@ -410,7 +410,7 @@ def tile_list_cocitation_drift_backward_kernel(
         weave(3, 1)
         for g in (1, 0):
             quantise_y(3, g)
-            store_codes(3, slice(g, g + 1))
+        store_codes(3)
 
         sc_rows = out_2.bitcast(I32).rearrange("g (q r) c -> r q g c", r=4)
         for r in range(4):

from contextlib import ExitStack

import concourse.mybir as mybir

K, H, N, T, S = 1024, 512, 1024, 4096, 1024
FLOPS = 2 * K * H * S * 2 + 2 * H * N * S

F32 = mybir.dt.float32
BF16 = mybir.dt.bfloat16
I32 = mybir.dt.int32
U32 = mybir.dt.uint32
U16 = mybir.dt.uint16
U8 = mybir.dt.uint8
FP8X4 = mybir.dt.float8_e4m3fn_x4
FP4X4 = mybir.dt.float4_e2m1fn_x4
ACT = mybir.ActivationFunctionType
ALU = mybir.AluOpType

P = 128
PACK = 4
GROUP = P * PACK
PASSES = K // GROUP
GROUPS = N // GROUP
HALF = S // 2
QUARTER = S // 4
BLOCK = 128
SHIFT = 16
ALIGN = 64

TILES = {
    "tab_sc": (U8, 1, [T]),
    "wb_sc_raw": (U8, 1, [PASSES * H]),
    "wd_sc_raw": (U8, 1, [N]),
    "v_sc_hi": (U8, 1, [2 * S]),
    "gain_raw": (F32, 4, [GROUPS, PACK]),
    "neg_gain": (F32, 4, [GROUPS * PACK]),
    "bias": (F32, 4, [PACK]),
    "w1_first": (F32, 4, [PACK // 2, H]),
    "w1_second": (F32, 4, [PACK // 2, H]),
    "w1_third": (F32, 4, [PACK, H // 2]),
    "w1_fourth": (F32, 4, [PACK, H // 2]),
    "wd_raw": (I32, 4, [N // 2]),
    "wd": (U16, 2, [N]),
    "wb_sc": (U8, 1, [PASSES * H]),
    "y_sc": (U8, 1, [GROUPS * S]),
    **{"tab%d" % a: (U16, 2, [T]) for a in range(PASSES)},
    **{"w1_bf%d" % a: (BF16, 2, [PACK, P, PACK]) for a in range(PASSES)},
    **{"w1_codes%d" % a: (U32, 4, [H]) for a in range(PASSES)},
    **{"w1_sc%d" % a: (U8, 1, [H]) for a in range(PASSES)},
    **{"wb_raw%d" % a: (I32, 4, [H]) for a in range(PASSES)},
    **{"wb%d" % a: (I32, 4, [H]) for a in range(PASSES)},
    **{"wd_sc%d" % g: (U8, 1, [GROUP]) for g in range(GROUPS)},
    **{"v_sc_lo%d" % n: (U8, 1, [S]) for n in range(2)},
    **{"v%d%d%d" % (n, a, h): (U16, 2, [HALF]) for n in range(2) for a in range(PASSES) for h in range(2)},
    **{"tanh%d" % h: (F32, 4, [PACK, HALF]) for h in range(2)},
    **{"sq%d%d" % (q, b): (F32, 4, [BLOCK, PACK]) for q in range(4) for b in range(2)},
    **{"neg_h%d" % q: (BF16, 2, [QUARTER * PACK]) for q in range(4)},
    **{"h_codes%d" % q: (U32, 4, [QUARTER]) for q in range(4)},
    **{"h_sc%d" % q: (U8, 1, [QUARTER]) for q in range(4)},
    **{"y%d%d" % (q, g): (F32, 4, [PACK, QUARTER]) for q in range(4) for g in range(GROUPS)},
    **{"y_bf%d%d" % (q, g): (BF16, 2, [QUARTER * PACK]) for q in range(4) for g in range(GROUPS)},
    **{"y_codes%d" % q: (U32, 4, [GROUPS * QUARTER]) for q in range(4)},
}

HEIRS = {
    "gain_raw": ["bias", "w1_second", "tab0", "w1_third", "w1_fourth", "tab1", "wd_raw"],
    "w1_second": ["v001", "wb_raw0", "wb_raw1"],
    "wb_raw1": ["wd_sc1", "sq10"],
    "wd_raw": ["tanh0"],
    "w1_bf0": ["wb_sc"],
    "w1_bf1": ["wd_sc0"],
    "v010": ["v100", "v101"],
    "sq01": ["v111"],
    "neg_h0": ["sq11"],
    "sq11": ["sq20", "y_bf00"],
    "h_codes0": ["sq21"],
    "sq21": ["y_bf01", "y_codes0"],
    "h_sc1": ["sq30", "sq31"],
    "y_bf00": ["neg_h3"],
    "sq31": ["y_bf10", "y_bf11", "y_bf20"],
    "h_sc3": ["y_bf30"],
}


def elements(name):
    count = 1
    for size in TILES[name][2]:
        count = count * size
    return count


def span(name):
    own = -(-elements(name) * TILES[name][1] // ALIGN) * ALIGN
    return max(own, sum(span(heir) for heir in HEIRS.get(name, [])))


def lay_out(names, start):
    places = {}
    for name in names:
        places[name] = start
        places.update(lay_out(HEIRS.get(name, []), start))
        start = start + span(name)
    return places


def tile_list_cocitation_drift_backward_kernel(
    tc, tab_words, tab_scales, offs, offs2, w1, b1, wb_words, wb_scales, wd_words, wd_scales, gain,
    out_0, out_1, out_2,
):
    nc = tc.nc
    heirs = [heir for names in HEIRS.values() for heir in names]
    places = lay_out([name for name in TILES if name not in heirs], 0)
    with ExitStack() as ctx:
        lists = ctx.enter_context(tc.tile_pool(name="lists", bufs=1))
        pool = ctx.enter_context(tc.tile_pool(name="pool", bufs=1))
        psum = ctx.enter_context(tc.psum_pool(name="psum", bufs=1))
        made = {}

        def sb(name):
            if name not in made:
                dtype, width, shape = TILES[name]
                tile = pool.tile([P, span(name) // width], dtype, name=name, offset=places[name], align_bytes=ALIGN)
                view = tile[:, : elements(name)]
                if len(shape) == 2:
                    view = view.rearrange("p (a b) -> p a b", a=shape[0])
                if len(shape) == 3:
                    view = view.rearrange("p (a b c) -> p a b c", a=shape[0], b=shape[1])
                made[name] = view
            return made[name]

        idx = [lists.tile([P, S // 16], U16, name="idx%d" % n) for n in range(2)]

        for name in ("tab_sc", "wb_sc_raw", "wd_sc_raw", "v_sc_hi"):
            nc.vector.memset(sb(name).bitcast(I32), 0)

        nc.sync.dma_start(sb("gain_raw"), gain.rearrange("(g p t) -> p g t", p=P, t=PACK))
        nc.sync.dma_start(idx[0][:], offs)
        nc.sync.dma_start(idx[1][:], offs2)
        tab_rows = tab_scales.bitcast(I32).rearrange("a (q r) c -> r q a c", r=4)
        for r in range(4):
            nc.sync.dma_start(sb("tab_sc").bitcast(I32)[r:P:SHIFT, :], tab_rows[r])

        wb_rows = wb_scales.bitcast(I32).rearrange("a (q r) c -> r q a c", r=4)
        wd_rows = wd_scales[0].bitcast(I32).rearrange("(q r) c -> r q c", r=4)
        for r in range(4):
            nc.gpsimd.dma_start(
                sb("wb_sc_raw").bitcast(I32)[r:P:32, :].rearrange("q (a c) -> q a c", a=PASSES), wb_rows[r]
            )
        for r in range(4):
            nc.gpsimd.dma_start(sb("wd_sc_raw").bitcast(I32)[r:P:32, :], wd_rows[r])

        nc.scalar.activation(
            sb("neg_gain").rearrange("p (g t) -> p g t", t=PACK), sb("gain_raw"), ACT.Copy, scale=-1.0
        )

        w1_rows = w1.rearrange("(a p j) c -> a p j c", p=P, j=PACK)

        def load_w1(a, name, rows, columns):
            nc.sync.dma_start(sb(name), w1_rows[a][:, rows, columns])
            nc.scalar.activation(
                sb("w1_bf%d" % a)[:, :, columns.start // PACK : columns.stop // PACK, rows].rearrange(
                    "p t m j -> p m j t"
                ),
                sb(name).rearrange("p j (m t) -> p m j t", t=PACK),
                ACT.Copy,
            )

        def quantise_w1(a):
            nc.vector.quantize_mx(
                out=sb("w1_codes%d" % a).bitcast(FP8X4),
                scales=sb("w1_sc%d" % a),
                in_=sb("w1_bf%d" % a).rearrange("p t m j -> p (t m j)"),
            )

        def load_table(a):
            nc.sync.dma_start(sb("tab%d" % a).bitcast(I32), tab_words[a].bitcast(I32))

        load_w1(0, "w1_first", slice(0, PACK // 2), slice(0, H))
        load_w1(0, "w1_second", slice(PACK // 2, PACK), slice(0, H))
        load_table(0)
        load_w1(1, "w1_third", slice(0, PACK), slice(0, H // 2))
        load_w1(1, "w1_fourth", slice(0, PACK), slice(H // 2, H))
        load_table(1)
        nc.sync.dma_start(sb("bias"), b1.rearrange("(p t) -> p t", t=PACK))
        nc.sync.dma_start(sb("wd_raw"), wd_words[0].bitcast(I32))

        v_sc = []
        for n in range(2):
            v_sc_lo = sb("v_sc_lo%d" % n)
            nc.vector.tensor_copy(v_sc_lo, sb("tab_sc").indirect(idx[n][:]))
            moved = sb("v_sc_hi")[:, n * S : (n + 1) * S]
            nc.sync.dma_start(moved.bitcast(I32)[0 : P - SHIFT, :], v_sc_lo.bitcast(I32)[SHIFT:P, :])
            v_sc.append((v_sc_lo, moved))

        def deal(out, in_, copy=nc.gpsimd.tensor_copy):
            copy(
                out.rearrange("p (u t m) -> p u t m", t=PACK, m=P),
                in_.rearrange("p (u m t) -> p u t m", t=PACK, m=P),
            )

        def gather(n, a, half):
            columns = slice(half * HALF // 16, (half + 1) * HALF // 16)
            nc.vector.tensor_copy(sb("v%d%d%d" % (n, a, half)), sb("tab%d" % a).indirect(idx[n][:, columns]))

        def bank(number, shape, name):
            return psum.tile([P] + shape, F32, name=name, tag="bank%d" % number)

        pre = {}

        def hidden(half, order, banks):
            for t in range(PACK):
                pre[half, t] = bank(banks[t], [HALF], "pre%d%d" % (half, t))
            for a, t in order:
                units = slice(t * P, (t + 1) * P)
                nc.tensor.matmul_mx(
                    out=pre[half, t][:],
                    lhsT=sb("w1_codes%d" % a)[:, units].bitcast(FP8X4),
                    lhsT_scale=sb("w1_sc%d" % a)[:, units],
                    rhs=sb("v0%d%d" % (a, half)).bitcast(FP4X4),
                    rhs_scale=v_sc[0][a][:, half * HALF : (half + 1) * HALF],
                    start=(a == 0),
                    stop=(a == PASSES - 1),
                )

        def take_tanh(half, slices=range(PACK)):
            for t in slices:
                nc.scalar.activation(
                    sb("tanh%d" % half)[:, t, :], pre[half, t][:], ACT.Tanh, bias=sb("bias")[:, t : t + 1]
                )

        def tanh_block(q, b):
            half, part = divmod(q, 2)
            first = part * QUARTER + b * BLOCK
            return sb("tanh%d" % half)[:, :, first : first + BLOCK]

        def square(q, b):
            nc.scalar.activation(
                sb("sq%d%d" % (q, b)).rearrange("p (c i) t -> p c t i", i=4),
                tanh_block(q, b).rearrange("p t (c i) -> p c t i", i=4),
                ACT.Square,
            )

        def square_on_vector(q, b):
            rows = tanh_block(q, b).rearrange("p t (c i) -> p c t i", i=4)
            nc.vector.tensor_tensor(sb("sq%d%d" % (q, b)).rearrange("p (c i) t -> p c t i", i=4), rows, rows, ALU.mult)

        def square_on_gpsimd(q, b):
            rows = tanh_block(q, b).rearrange("p t j -> p j t")
            nc.gpsimd.tensor_tensor(sb("sq%d%d" % (q, b)), rows, rows, ALU.mult)

        err = {}

        def errors(q, banks, passes=(0, 1)):
            half, part = divmod(q, 2)
            for b in range(2):
                inside = part * QUARTER + b * BLOCK
                first = half * HALF + inside
                err[q, b] = bank(banks[b], [PACK, BLOCK], "err%d%d" % (q, b))
                for a in passes:
                    for t in range(PACK):
                        nc.tensor.matmul_mx(
                            out=err[q, b][:, t, :],
                            lhsT=sb("wb%d" % a)[:, t * P : (t + 1) * P].bitcast(FP8X4),
                            lhsT_scale=sb("wb_sc")[:, a * H + t * P : a * H + (t + 1) * P],
                            rhs=sb("v1%d%d" % (a, half))[:, inside : inside + BLOCK].bitcast(FP4X4),
                            rhs_scale=v_sc[1][a][:, first : first + BLOCK],
                            start=(a == passes[0] and t == 0),
                            stop=(a == passes[-1] and t == PACK - 1),
                        )

        def make_h(q):
            neg_h = sb("neg_h%d" % q)
            for b in range(2):
                nc.vector.scalar_tensor_tensor(
                    out=neg_h[:, b * BLOCK * PACK : (b + 1) * BLOCK * PACK].rearrange("p (j t) -> p j t", t=PACK),
                    in0=sb("sq%d%d" % (q, b)),
                    scalar=1.0,
                    in1=err[q, b][:].rearrange("p t j -> p j t"),
                    op0=ALU.subtract,
                    op1=ALU.mult,
                )
            for b in range(2):
                nc.vector.quantize_mx(
                    out=sb("h_codes%d" % q)[:, b * BLOCK : (b + 1) * BLOCK].bitcast(FP8X4),
                    scales=sb("h_sc%d" % q)[:, b * BLOCK : (b + 1) * BLOCK],
                    in_=neg_h[:, b * BLOCK * PACK : (b + 1) * BLOCK * PACK],
                )

        y_rows = out_0.rearrange("(g p t) j -> g p t j", p=P, t=PACK)
        y_words = out_1.rearrange("g p m t -> p g (m t)").bitcast(I32)
        acc = {}

        def multiply_y(q, g, banks):
            for pair in range(PACK // 2):
                acc[q, g, pair] = bank(banks[pair], [2, QUARTER], "acc%d%d%d" % (q, g, pair))
                for u in range(2):
                    first = (2 * pair + u) * P
                    nc.tensor.matmul_mx(
                        out=acc[q, g, pair][:, u, :],
                        lhsT=sb("wd")[:, g * GROUP + first : g * GROUP + first + P].bitcast(FP4X4),
                        lhsT_scale=sb("wd_sc%d" % g)[:, first : first + P],
                        rhs=sb("h_codes%d" % q).bitcast(FP8X4),
                        rhs_scale=sb("h_sc%d" % q),
                        start=True,
                        stop=True,
                    )

        def empty_y(q, g):
            y = sb("y%d%d" % (q, g))
            for t in range(PACK):
                factor = sb("neg_gain")[:, g * PACK + t : g * PACK + t + 1]
                nc.scalar.activation(y[:, t, :], acc[q, g, t // 2][:, t % 2, :], ACT.Copy, scale=factor)
                if t % 2 == 1:
                    rows = slice(t - 1, t + 1)
                    nc.sync.dma_start(y_rows[g][:, rows, q * QUARTER : (q + 1) * QUARTER], y[:, rows, :])

        def weave(q, g, copies=(nc.vector.tensor_copy,)):
            width = QUARTER // len(copies)
            for n, copy in enumerate(copies):
                copy(
                    sb("y_bf%d%d" % (q, g))[:, n * width * PACK : (n + 1) * width * PACK].rearrange(
                        "p (c i t) -> p c t i", i=4, t=PACK
                    ),
                    sb("y%d%d" % (q, g))[:, :, n * width : (n + 1) * width].rearrange("p t (c i) -> p c t i", i=4),
                )

        def quantise_y(q, g):
            nc.vector.quantize_mx(
                out=sb("y_codes%d" % q)[:, g * QUARTER : (g + 1) * QUARTER].bitcast(FP8X4),
                scales=sb("y_sc")[:, g * S + q * QUARTER : g * S + (q + 1) * QUARTER],
                in_=sb("y_bf%d%d" % (q, g)),
            )

        def store_codes(q):
            nc.sync.dma_start(
                y_words[:, :, q * QUARTER : (q + 1) * QUARTER],
                sb("y_codes%d" % q).bitcast(I32).rearrange("p (g m) -> p g m", g=GROUPS),
            )

        def make_y(q, g, banks):
            multiply_y(q, g, banks)
            empty_y(q, g)

        def make_planes(q):
            weave(q, 0)
            weave(q, 1)
            quantise_y(q, 0)
            quantise_y(q, 1)
            store_codes(q)

        quantise_w1(0)
        gather(0, 0, 0)
        gather(0, 0, 1)
        quantise_w1(1)
        gather(0, 1, 0)
        gather(0, 1, 1)
        gather(1, 1, 0)

        def deal_wd_scales(g):
            deal(sb("wd_sc%d" % g), sb("wd_sc_raw")[:, g * GROUP : (g + 1) * GROUP])

        deal(sb("wb_sc"), sb("wb_sc_raw"))
        deal_wd_scales(0)
        for a in range(PASSES):
            nc.sync.dma_start(sb("wb_raw%d" % a), wb_words[a].rearrange("p c i -> p (c i)").bitcast(I32))
            deal(sb("wb%d" % a), sb("wb_raw%d" % a))
        deal_wd_scales(1)
        hidden(0, [(a, t) for a in range(PASSES) for t in range(PACK)], (0, 1, 2, 3))
        gather(1, 0, 0)
        gather(1, 0, 1)
        deal(sb("wd"), sb("wd_raw").bitcast(U16), nc.scalar.copy)

        take_tanh(0)
        hidden(1, [(a, t) for t in range(PACK) for a in range(PASSES)], (0, 1, 4, 5))
        take_tanh(1, range(1))
        square(0, 0)
        square(0, 1)
        square_on_gpsimd(1, 0)
        take_tanh(1, range(1, PACK))
        errors(0, (2, 3), (1, 0))
        make_h(0)
        square_on_gpsimd(1, 1)
        make_y(0, 0, (2, 3))
        make_y(0, 1, (0, 1))
        gather(1, 1, 1)
        errors(1, (6, 7), (1, 0))
        make_h(1)
        square(2, 1)
        square_on_vector(2, 0)
        weave(0, 0)
        make_y(1, 0, (4, 5))
        make_y(1, 1, (2, 3))
        errors(2, (6, 7))
        square(3, 0)
        square(3, 1)
        make_h(2)
        weave(0, 1)
        quantise_y(0, 0)
        quantise_y(0, 1)
        store_codes(0)
        errors(3, (6, 7))
        make_y(2, 0, (0, 1))
        make_h(3)
        make_y(2, 1, (6, 7))
        make_y(3, 0, (4, 5))
        make_y(3, 1, (2, 3))
        make_planes(1)
        make_planes(2)
        weave(3, 0, (nc.scalar.copy,))
        weave(3, 1)
        for g in (1, 0):
            quantise_y(3, g)
        store_codes(3)

        sc_rows = out_2.bitcast(I32).rearrange("g (q r) c -> r q g c", r=4)
        for r in range(4):
            queue = nc.sync if r % 2 == 0 else nc.scalar
            queue.dma_start(
                sc_rows[r], sb("y_sc").bitcast(I32)[r:P:32, :].rearrange("q (g c) -> q g c", g=GROUPS)
            )
